import numpy as np
import ml_dtypes


def mxq(x, axis, fmt="e4m3"):
    dtype, down = {"e4m3": (ml_dtypes.float8_e4m3fn, 7), "e5m2": (ml_dtypes.float8_e5m2, 14)}[fmt]
    v = np.moveaxis(np.asarray(x, np.float32).astype(ml_dtypes.bfloat16).astype(np.float64), axis, -1)
    blocks = v.reshape(v.shape[:-1] + (-1, 32))
    amax = np.abs(blocks).max(-1, keepdims=True)
    byte = np.maximum(np.where(amax > 0, np.frexp(amax)[1] - 1 + 127, 0) - down, 1)
    scale = np.exp2(byte - 127.0)
    codes = (blocks / scale).astype(np.float32).astype(dtype).astype(np.float64)
    return np.moveaxis((codes * scale).reshape(v.shape), -1, axis)


WIDE = False


def mx_kscale(k):
    if not WIDE:
        return np.ones(k)
    levels = np.array([10, -10, 5, -5, 0])
    if k % 512:
        return np.exp2(np.random.permutation(np.resize(levels, k // 32))).repeat(32)
    a = np.empty((k // 512, 16))
    for p in range(k // 512):
        a[p, :8] = np.random.permutation(np.resize(levels, 8))
        for g in range(8):
            far = levels[np.abs(levels - a[p, g]) >= 10]
            a[p, g + 8] = far[np.random.randint(len(far))]
    return np.exp2(a.ravel()).repeat(32)


def f64(x):
    return np.asarray(x).astype(np.float64)


def striped(idx):
    return np.tile(idx.reshape(-1, 16).T, (8, 1)).astype(np.uint16)


def unstriped(offs):
    return offs[:16].T.reshape(-1).astype(np.int64)


def pack_weight(w):
    k, n = w.shape
    w = f64(np.asarray(w, np.float32).astype(ml_dtypes.bfloat16)).reshape(k // 32, 32, n)
    amax = np.abs(w).max(1)
    byte = np.clip(np.where(amax > 0, np.frexp(amax)[1] - 1 + 127 - 7, 1), 1, 254)
    scaled = (w * np.exp2(127.0 - byte)[:, None, :]).reshape(k, n).astype(np.float32)
    words = np.ascontiguousarray(scaled.reshape(k // 512, 128, 4, n).transpose(0, 1, 3, 2)).astype(ml_dtypes.float8_e4m3fn).view(np.uint8)
    return words, np.ascontiguousarray(byte.astype(np.uint8).reshape(k // 512, 16, n))


def unpack_weight(words, scales):
    g, p, n, _ = words.shape
    vals = np.ascontiguousarray(words).view(ml_dtypes.float8_e4m3fn).astype(np.float64) * np.repeat(np.exp2(scales.astype(np.float64) - 127.0), 8, axis=1)[..., None]
    return vals.transpose(0, 1, 3, 2).reshape(g * 512, n)


K, T, S, V, N, D = 512, 2048, 512, 256, 256, 2
P = 2 ** 7


def setup_inputs():
    n = np.random.standard_normal
    s = mx_kscale(K)[:, None]
    packed_xT = pack_weight(n((K, T)) * s)
    return {
        "x_words": packed_xT[0],
        "x_scales": packed_xT[1],
        "w1": (n((K, N)) / np.sqrt(K) / s).astype(np.float32),
        "wgt": (np.tile(np.random.uniform(0.5, 2.0, (D, 1, V)), (1, P, 1))).astype(np.float32),
        "offs": striped(np.random.permutation(T)[:S]),
        "case": striped(np.random.permutation(S)[:V]),
        "pos1": striped(np.random.permutation(S)[:V]),
        "pos2": striped(np.random.permutation(S)[:V]),
    }


def reference(x_words, x_scales, w1, wgt, offs, case, pos1, pos2):
    xq = unpack_weight(x_words, x_scales)[:, unstriped(offs)]
    y = mxq(f64(w1), 0, "e4m3").T @ xq
    yc = y[:, unstriped(case)]
    ec = np.exp(yc)
    den = ec + (np.exp(y[:, unstriped(pos1)])) * f64(wgt)[0, :1] + (np.exp(y[:, unstriped(pos2)])) * f64(wgt)[1, :1]
    return np.log(den) - yc

@@ -1,0 +1,140 @@
+from contextlib import ExitStack
+
+import concourse.mybir as mybir
+
+K, T, S, V, N, D = 512, 2048, 512, 256, 256, 2
+P = 128
+PACK = 4
+HALF = S // 2
+FLOPS = 2 * K * N * S
+
+F32 = mybir.dt.float32
+BF16 = mybir.dt.bfloat16
+I32 = mybir.dt.int32
+U32 = mybir.dt.uint32
+U16 = mybir.dt.uint16
+U8 = mybir.dt.uint8
+FP8X4 = mybir.dt.float8_e4m3fn_x4
+ALU = mybir.AluOpType
+ACT = mybir.ActivationFunctionType
+
+
+def tile_picked_ycox_nll_p_kernel(
+    tc, x_words, x_scales, w1, wgt, offs, case, pos1, pos2, out
+):
+    nc = tc.nc
+    blocks = range(N // P)
+    with ExitStack() as ctx:
+        keep = ctx.enter_context(tc.tile_pool(name="keep", bufs=1))
+        psum = ctx.enter_context(tc.psum_pool(name="psum", bufs=1))
+        shared = ctx.enter_context(tc.tile_pool(name="shared", bufs=1))
+
+        scale_table = shared.tile([P, T], U8, name="scale_table", align_bytes=64, offset=0)
+        nc.vector.memset(scale_table[:].bitcast(I32), 0)
+        for q in range(4):
+            nc.scalar.dma_start(
+                out=scale_table[32 * q : 32 * q + 4, :].bitcast(I32),
+                in_=x_scales[0, 4 * q : 4 * q + 4, :].bitcast(I32),
+            )
+
+        offs_sb = keep.tile([P, S // 16], U16, name="offs_sb")
+        nc.sync.dma_start(offs_sb[:], offs)
+        w_raw = keep.tile([P, PACK, N], F32, name="w_raw")
+        nc.sync.dma_start(out=w_raw[:], in_=w1.rearrange("(p j) m -> p j m", j=PACK))
+        word_table = keep.tile([P, T], U32, name="word_table", align_bytes=64)
+        nc.sync.dma_start(
+            out=word_table[:].bitcast(I32),
+            in_=x_words[0].rearrange("p c r -> p (c r)").bitcast(I32),
+        )
+        case_sb = keep.tile([P, V // 16], U16, name="case_sb")
+        nc.sync.dma_start(case_sb[:], case)
+        pos_sb = []
+        for d, pos in enumerate((pos1, pos2)):
+            pos_d = keep.tile([P, V // 16], U16, name="pos_sb%d" % d)
+            nc.sync.dma_start(pos_d[:], pos)
+            pos_sb.append(pos_d)
+        wgt_sb = keep.tile([P, D, V], F32, name="wgt_sb")
+        nc.sync.dma_start(out=wgt_sb[:], in_=wgt.rearrange("d p v -> p d v"))
+
+        x_scale = keep.tile([P, S], U8, name="x_scale", align_bytes=64)
+        nc.vector.tensor_copy(x_scale[:], scale_table[:].indirect(offs_sb[:]))
+
+        w_bf = shared.tile([P, N, PACK], BF16, name="w_bf", align_bytes=64, offset=2048)
+        nc.scalar.activation(w_bf[:], w_raw[:].rearrange("p j m -> p m j"), ACT.Copy)
+        w_code = shared.tile([P, N], U32, name="w_code", align_bytes=64, offset=0)
+        w_scale = keep.tile([P, N], U8, name="w_scale", align_bytes=64)
+        nc.vector.quantize_mx(
+            out=w_code[:].bitcast(FP8X4),
+            scales=w_scale[:],
+            in_=w_bf[:].rearrange("p m j -> p (m j)"),
+        )
+
+        y = [keep.tile([P, S], F32, name="y%d" % b) for b in blocks]
+        x_code = []
+        for h in range(2):
+            code_h = shared.tile([P, HALF], U32, name="x_code%d" % h, align_bytes=64, offset=(2 + h) * 1024)
+            nc.vector.tensor_copy(
+                code_h[:], word_table[:].indirect(offs_sb[:, h * HALF // 16 : (h + 1) * HALF // 16])
+            )
+            x_code.append(code_h)
+        for b in blocks:
+            rows = slice(b * P, (b + 1) * P)
+            for h in range(2):
+                cols = slice(h * HALF, (h + 1) * HALF)
+                acc = psum.tile([P, HALF], F32, name="acc%d%d" % (b, h))
+                nc.tensor.matmul_mx(
+                    out=acc[:],
+                    lhsT=w_code[:, rows].bitcast(FP8X4),
+                    lhsT_scale=w_scale[:, rows],
+                    rhs=x_code[h][:].bitcast(FP8X4),
+                    rhs_scale=x_scale[:, cols],
+                    start=True,
+                    stop=True,
+                )
+                nc.scalar.activation(y[b][:, cols], acc[:], ACT.Copy)
+
+        def fresh(label, b):
+            return keep.tile([P, V], F32, name="%s%d" % (label, b))
+
+        top, e_case, e_ctl = [], [], []
+        for b in blocks:
+            yc = fresh("yc", b)
+            nc.vector.tensor_copy(yc[:], y[b][:].indirect(case_sb[:]))
+            diff = []
+            for d in range(D):
+                diff_d = fresh("diff%d" % d, b)
+                nc.vector.tensor_tensor(diff_d[:], y[b][:].indirect(pos_sb[d][:]), yc[:], ALU.subtract)
+                diff.append(diff_d)
+            top_b = fresh("top", b)
+            nc.vector.scalar_tensor_tensor(top_b[:], diff[0][:], 0.0, diff[1][:], ALU.max, ALU.max)
+            top.append(top_b)
+            e0 = fresh("e_case", b)
+            nc.scalar.activation(e0[:], top_b[:], ACT.Exp, scale=-1.0)
+            e_case.append(e0)
+            e_b = keep.tile([P, D, V], F32, name="e_ctl%d" % b)
+            for d in range(D):
+                shifted = fresh("shifted%d" % d, b)
+                nc.vector.tensor_tensor(shifted[:], diff[d][:], top_b[:], ALU.subtract)
+                nc.scalar.activation(e_b[:, d, :], shifted[:], ACT.Exp)
+            e_ctl.append(e_b)
+
+        warm = keep.tile([P, 1], F32, name="warm")
+        nc.scalar.activation(warm[:], e_ctl[-1][:, D - 1, 0:1], ACT.Ln, bias=1.0)
+
+        den, weighted_all = [], []
+        for b in blocks:
+            weighted = keep.tile([P, D, V], F32, name="weighted%d" % b)
+            nc.vector.tensor_tensor(weighted[:], e_ctl[b][:], wgt_sb[:], ALU.mult)
+            part = fresh("part", b)
+            nc.vector.tensor_tensor(part[:], weighted[:, 0, :], e_case[b][:], ALU.add)
+            den_b = fresh("den", b)
+            nc.vector.tensor_tensor(den_b[:], weighted[:, 1, :], part[:], ALU.add)
+            den.append(den_b)
+            weighted_all.append(weighted)
+
+        for b in blocks:
+            log_den = fresh("log_den", b)
+            nc.scalar.activation(log_den[:], den[b][:], ACT.Ln)
+            result = weighted_all[-1][:, D - 1 - b, :]
+            nc.vector.tensor_tensor(result, log_den[:], top[b][:], ALU.add)
+            nc.sync.dma_start(out=out[b * P : (b + 1) * P, :], in_=result)

@@ -39,13 +39,16 @@ def tile_picked_ycox_nll_p_kernel(
 
         offs_sb = keep.tile([P, S // 16], U16, name="offs_sb")
         nc.sync.dma_start(offs_sb[:], offs)
-        w_raw = keep.tile([P, PACK, N], F32, name="w_raw")
-        nc.sync.dma_start(out=w_raw[:], in_=w1.rearrange("(p j) m -> p j m", j=PACK))
         word_table = keep.tile([P, T], U32, name="word_table", align_bytes=64)
         nc.sync.dma_start(
             out=word_table[:].bitcast(I32),
             in_=x_words[0].rearrange("p c r -> p (c r)").bitcast(I32),
         )
+        w_raw = [keep.tile([P, PACK, P], F32, name="w_raw%d" % b) for b in blocks]
+        for b in blocks:
+            nc.sync.dma_start(
+                out=w_raw[b][:], in_=w1[:, b * P : (b + 1) * P].rearrange("(p j) m -> p j m", j=PACK)
+            )
         case_sb = keep.tile([P, V // 16], U16, name="case_sb")
         nc.sync.dma_start(case_sb[:], case)
         pos_sb = []
@@ -59,33 +62,37 @@ def tile_picked_ycox_nll_p_kernel(
         x_scale = keep.tile([P, S], U8, name="x_scale", align_bytes=64)
         nc.vector.tensor_copy(x_scale[:], scale_table[:].indirect(offs_sb[:]))
 
-        w_bf = shared.tile([P, N, PACK], BF16, name="w_bf", align_bytes=64, offset=2048)
-        nc.scalar.activation(w_bf[:], w_raw[:].rearrange("p j m -> p m j"), ACT.Copy)
-        w_code = shared.tile([P, N], U32, name="w_code", align_bytes=64, offset=0)
-        w_scale = keep.tile([P, N], U8, name="w_scale", align_bytes=64)
-        nc.vector.quantize_mx(
-            out=w_code[:].bitcast(FP8X4),
-            scales=w_scale[:],
-            in_=w_bf[:].rearrange("p m j -> p (m j)"),
-        )
-
-        y = [keep.tile([P, S], F32, name="y%d" % b) for b in blocks]
         x_code = []
         for h in range(2):
-            code_h = shared.tile([P, HALF], U32, name="x_code%d" % h, align_bytes=64, offset=(2 + h) * 1024)
+            code_h = shared.tile([P, HALF], U32, name="x_code%d" % h, align_bytes=64, offset=h * 1024)
             nc.vector.tensor_copy(
                 code_h[:], word_table[:].indirect(offs_sb[:, h * HALF // 16 : (h + 1) * HALF // 16])
             )
             x_code.append(code_h)
+
+        w_code, w_scale = [], []
         for b in blocks:
-            rows = slice(b * P, (b + 1) * P)
+            w_bf = keep.tile([P, P, PACK], BF16, name="w_bf%d" % b, align_bytes=64)
+            nc.scalar.activation(w_bf[:], w_raw[b][:].rearrange("p j m -> p m j"), ACT.Copy)
+            code_b = keep.tile([P, P], U32, name="w_code%d" % b, align_bytes=64)
+            scale_b = keep.tile([P, P], U8, name="w_scale%d" % b, align_bytes=64)
+            nc.vector.quantize_mx(
+                out=code_b[:].bitcast(FP8X4),
+                scales=scale_b[:],
+                in_=w_bf[:].rearrange("p m j -> p (m j)"),
+            )
+            w_code.append(code_b)
+            w_scale.append(scale_b)
+
+        y = [keep.tile([P, S], F32, name="y%d" % b) for b in blocks]
+        for b in blocks:
             for h in range(2):
                 cols = slice(h * HALF, (h + 1) * HALF)
                 acc = psum.tile([P, HALF], F32, name="acc%d%d" % (b, h))
                 nc.tensor.matmul_mx(
                     out=acc[:],
-                    lhsT=w_code[:, rows].bitcast(FP8X4),
-                    lhsT_scale=w_scale[:, rows],
+                    lhsT=w_code[b][:].bitcast(FP8X4),
+                    lhsT_scale=w_scale[b][:],
                     rhs=x_code[h][:].bitcast(FP8X4),
                     rhs_scale=x_scale[:, cols],
                     start=True,
@@ -96,41 +103,37 @@ def tile_picked_ycox_nll_p_kernel(
         def fresh(label, b):
             return keep.tile([P, V], F32, name="%s%d" % (label, b))
 
-        top, e_case, e_ctl = [], [], []
+        diff = []
         for b in blocks:
             yc = fresh("yc", b)
             nc.vector.tensor_copy(yc[:], y[b][:].indirect(case_sb[:]))
-            diff = []
+            diff_b = [fresh("diff%d" % d, b) for d in range(D)]
             for d in range(D):
-                diff_d = fresh("diff%d" % d, b)
-                nc.vector.tensor_tensor(diff_d[:], y[b][:].indirect(pos_sb[d][:]), yc[:], ALU.subtract)
-                diff.append(diff_d)
-            top_b = fresh("top", b)
-            nc.vector.scalar_tensor_tensor(top_b[:], diff[0][:], 0.0, diff[1][:], ALU.max, ALU.max)
-            top.append(top_b)
-            e0 = fresh("e_case", b)
-            nc.scalar.activation(e0[:], top_b[:], ACT.Exp, scale=-1.0)
-            e_case.append(e0)
-            e_b = keep.tile([P, D, V], F32, name="e_ctl%d" % b)
+                nc.vector.tensor_tensor(diff_b[d][:], y[b][:].indirect(pos_sb[d][:]), yc[:], ALU.subtract)
+            diff.append(diff_b)
+
+        top = [fresh("top", b) for b in blocks]
+        e_case = [fresh("e_case", b) for b in blocks]
+        for b in blocks:
+            nc.vector.scalar_tensor_tensor(top[b][:], diff[b][0][:], 0.0, diff[b][1][:], ALU.max, ALU.max)
+            nc.scalar.activation(e_case[b][:], top[b][:], ACT.Exp, scale=-1.0)
+
+        e_ctl = [keep.tile([P, D, V], F32, name="e_ctl%d" % b) for b in blocks]
+        for b in blocks:
             for d in range(D):
                 shifted = fresh("shifted%d" % d, b)
-                nc.vector.tensor_tensor(shifted[:], diff[d][:], top_b[:], ALU.subtract)
-                nc.scalar.activation(e_b[:, d, :], shifted[:], ACT.Exp)
-            e_ctl.append(e_b)
+                nc.vector.tensor_tensor(shifted[:], diff[b][d][:], top[b][:], ALU.subtract)
+                nc.scalar.activation(e_ctl[b][:, d, :], shifted[:], ACT.Exp)
 
-        warm = keep.tile([P, 1], F32, name="warm")
-        nc.scalar.activation(warm[:], e_ctl[-1][:, D - 1, 0:1], ACT.Ln, bias=1.0)
-
-        den, weighted_all = [], []
+        weighted_all = [keep.tile([P, D, V], F32, name="weighted%d" % b) for b in blocks]
+        part = [fresh("part", b) for b in blocks]
+        den = [fresh("den", b) for b in blocks]
         for b in blocks:
-            weighted = keep.tile([P, D, V], F32, name="weighted%d" % b)
-            nc.vector.tensor_tensor(weighted[:], e_ctl[b][:], wgt_sb[:], ALU.mult)
-            part = fresh("part", b)
-            nc.vector.tensor_tensor(part[:], weighted[:, 0, :], e_case[b][:], ALU.add)
-            den_b = fresh("den", b)
-            nc.vector.tensor_tensor(den_b[:], weighted[:, 1, :], part[:], ALU.add)
-            den.append(den_b)
-            weighted_all.append(weighted)
+            nc.vector.tensor_tensor(weighted_all[b][:], e_ctl[b][:], wgt_sb[:], ALU.mult)
+        for b in blocks:
+            nc.vector.tensor_tensor(part[b][:], weighted_all[b][:, 0, :], e_case[b][:], ALU.add)
+        for b in blocks:
+            nc.vector.tensor_tensor(den[b][:], weighted_all[b][:, 1, :], part[b][:], ALU.add)
 
         for b in blocks:
             log_den = fresh("log_den", b)

@@ -31,24 +31,28 @@ def tile_picked_ycox_nll_p_kernel(
 
         scale_table = shared.tile([P, T], U8, name="scale_table", align_bytes=64, offset=0)
         nc.vector.memset(scale_table[:].bitcast(I32), 0)
+        w_raw = [keep.tile([P, PACK, P], F32, name="w_raw%d" % b) for b in blocks]
+
+        def load_w(b):
+            nc.sync.dma_start(
+                out=w_raw[b][:], in_=w1[:, b * P : (b + 1) * P].rearrange("(p j) m -> p j m", j=PACK)
+            )
+
+        load_w(0)
+        offs_sb = keep.tile([P, S // 16], U16, name="offs_sb")
+        nc.sync.dma_start(offs_sb[:], offs)
         for q in range(4):
-            nc.scalar.dma_start(
+            queue = nc.sync if q % 2 == 0 else nc.scalar
+            queue.dma_start(
                 out=scale_table[32 * q : 32 * q + 4, :].bitcast(I32),
                 in_=x_scales[0, 4 * q : 4 * q + 4, :].bitcast(I32),
             )
-
-        offs_sb = keep.tile([P, S // 16], U16, name="offs_sb")
-        nc.sync.dma_start(offs_sb[:], offs)
         word_table = keep.tile([P, T], U32, name="word_table", align_bytes=64)
         nc.sync.dma_start(
             out=word_table[:].bitcast(I32),
             in_=x_words[0].rearrange("p c r -> p (c r)").bitcast(I32),
         )
-        w_raw = [keep.tile([P, PACK, P], F32, name="w_raw%d" % b) for b in blocks]
-        for b in blocks:
-            nc.sync.dma_start(
-                out=w_raw[b][:], in_=w1[:, b * P : (b + 1) * P].rearrange("(p j) m -> p j m", j=PACK)
-            )
+        load_w(1)
         case_sb = keep.tile([P, V // 16], U16, name="case_sb")
         nc.sync.dma_start(case_sb[:], case)
         pos_sb = []
@@ -62,27 +66,33 @@ def tile_picked_ycox_nll_p_kernel(
         x_scale = keep.tile([P, S], U8, name="x_scale", align_bytes=64)
         nc.vector.tensor_copy(x_scale[:], scale_table[:].indirect(offs_sb[:]))
 
+        w_bf = [
+            shared.tile([P, P, PACK], BF16, name="w_bf0", align_bytes=64, offset=2048 + 512),
+            keep.tile([P, P, PACK], BF16, name="w_bf1", align_bytes=64),
+        ]
+        w_code = [
+            shared.tile([P, P], U32, name="w_code0", align_bytes=64, offset=0),
+            keep.tile([P, P], U32, name="w_code1", align_bytes=64),
+        ]
+        w_scale = [keep.tile([P, P], U8, name="w_scale%d" % b, align_bytes=64) for b in blocks]
+
+        def quantise_w(b):
+            nc.scalar.activation(w_bf[b][:], w_raw[b][:].rearrange("p j m -> p m j"), ACT.Copy)
+            nc.vector.quantize_mx(
+                out=w_code[b][:].bitcast(FP8X4),
+                scales=w_scale[b][:],
+                in_=w_bf[b][:].rearrange("p m j -> p (m j)"),
+            )
+
+        quantise_w(0)
         x_code = []
         for h in range(2):
-            code_h = shared.tile([P, HALF], U32, name="x_code%d" % h, align_bytes=64, offset=h * 1024)
+            code_h = shared.tile([P, HALF], U32, name="x_code%d" % h, align_bytes=64, offset=2048 + h * 1024)
             nc.vector.tensor_copy(
                 code_h[:], word_table[:].indirect(offs_sb[:, h * HALF // 16 : (h + 1) * HALF // 16])
             )
             x_code.append(code_h)
-
-        w_code, w_scale = [], []
-        for b in blocks:
-            w_bf = keep.tile([P, P, PACK], BF16, name="w_bf%d" % b, align_bytes=64)
-            nc.scalar.activation(w_bf[:], w_raw[b][:].rearrange("p j m -> p m j"), ACT.Copy)
-            code_b = keep.tile([P, P], U32, name="w_code%d" % b, align_bytes=64)
-            scale_b = keep.tile([P, P], U8, name="w_scale%d" % b, align_bytes=64)
-            nc.vector.quantize_mx(
-                out=code_b[:].bitcast(FP8X4),
-                scales=scale_b[:],
-                in_=w_bf[:].rearrange("p m j -> p (m j)"),
-            )
-            w_code.append(code_b)
-            w_scale.append(scale_b)
+        quantise_w(1)
 
         y = [keep.tile([P, S], F32, name="y%d" % b) for b in blocks]
         for b in blocks:
@@ -103,13 +113,24 @@ def tile_picked_ycox_nll_p_kernel(
         def fresh(label, b):
             return keep.tile([P, V], F32, name="%s%d" % (label, b))
 
+        def pieces(count):
+            width = V // count
+            return [
+                (slice(i * width, (i + 1) * width), slice(i * width // 16, (i + 1) * width // 16))
+                for i in range(count)
+            ]
+
         diff = []
         for b in blocks:
             yc = fresh("yc", b)
-            nc.vector.tensor_copy(yc[:], y[b][:].indirect(case_sb[:]))
+            for cases, entries in pieces(2 if b == 0 else 1):
+                nc.vector.tensor_copy(yc[:, cases], y[b][:].indirect(case_sb[:, entries]))
             diff_b = [fresh("diff%d" % d, b) for d in range(D)]
             for d in range(D):
-                nc.vector.tensor_tensor(diff_b[d][:], y[b][:].indirect(pos_sb[d][:]), yc[:], ALU.subtract)
+                for cases, entries in pieces(2 if (b, d) == (0, 0) else 1):
+                    nc.vector.tensor_tensor(
+                        diff_b[d][:, cases], y[b][:].indirect(pos_sb[d][:, entries]), yc[:, cases], ALU.subtract
+                    )
             diff.append(diff_b)
 
         top = [fresh("top", b) for b in blocks]
@@ -122,8 +143,9 @@ def tile_picked_ycox_nll_p_kernel(
         for b in blocks:
             for d in range(D):
                 shifted = fresh("shifted%d" % d, b)
-                nc.vector.tensor_tensor(shifted[:], diff[b][d][:], top[b][:], ALU.subtract)
-                nc.scalar.activation(e_ctl[b][:, d, :], shifted[:], ACT.Exp)
+                for cases, entries in pieces(2 if (b, d) == (1, 1) else 1):
+                    nc.vector.tensor_tensor(shifted[:, cases], diff[b][d][:, cases], top[b][:, cases], ALU.subtract)
+                    nc.scalar.activation(e_ctl[b][:, d, cases], shifted[:, cases], ACT.Exp)
 
         weighted_all = [keep.tile([P, D, V], F32, name="weighted%d" % b) for b in blocks]
         part = [fresh("part", b) for b in blocks]
@@ -137,7 +159,8 @@ def tile_picked_ycox_nll_p_kernel(
 
         for b in blocks:
             log_den = fresh("log_den", b)
-            nc.scalar.activation(log_den[:], den[b][:], ACT.Ln)
             result = weighted_all[-1][:, D - 1 - b, :]
-            nc.vector.tensor_tensor(result, log_den[:], top[b][:], ALU.add)
+            for cases, entries in pieces(2):
+                nc.scalar.activation(log_den[:, cases], den[b][:, cases], ACT.Ln)
+                nc.vector.tensor_tensor(result[:, cases], log_den[:, cases], top[b][:, cases], ALU.add)
             nc.sync.dma_start(out=out[b * P : (b + 1) * P, :], in_=result)

@@ -95,20 +95,29 @@ def tile_picked_ycox_nll_p_kernel(
         quantise_w(1)
 
         y = [keep.tile([P, S], F32, name="y%d" % b) for b in blocks]
-        for b in blocks:
-            for h in range(2):
-                cols = slice(h * HALF, (h + 1) * HALF)
-                acc = psum.tile([P, HALF], F32, name="acc%d%d" % (b, h))
-                nc.tensor.matmul_mx(
-                    out=acc[:],
-                    lhsT=w_code[b][:].bitcast(FP8X4),
-                    lhsT_scale=w_scale[b][:],
-                    rhs=x_code[h][:].bitcast(FP8X4),
-                    rhs_scale=x_scale[:, cols],
-                    start=True,
-                    stop=True,
-                )
+
+        def product(b, h, start, width, on_vector=False):
+            cols = slice(h * HALF + start, h * HALF + start + width)
+            acc = psum.tile([P, width], F32, name="acc%d_%d" % (b, cols.start))
+            nc.tensor.matmul_mx(
+                out=acc[:],
+                lhsT=w_code[b][:].bitcast(FP8X4),
+                lhsT_scale=w_scale[b][:],
+                rhs=x_code[h][:, start : start + width].bitcast(FP8X4),
+                rhs_scale=x_scale[:, cols],
+                start=True,
+                stop=True,
+            )
+            if on_vector:
+                nc.vector.tensor_copy(y[b][:, cols], acc[:])
+            else:
                 nc.scalar.activation(y[b][:, cols], acc[:], ACT.Copy)
+
+        product(0, 0, 0, HALF)
+        product(0, 1, 0, P)
+        product(0, 1, P, P, on_vector=True)
+        product(1, 0, 0, HALF)
+        product(1, 1, 0, HALF)
 
         def fresh(label, b):
             return keep.tile([P, V], F32, name="%s%d" % (label, b))
@@ -155,7 +164,8 @@ def tile_picked_ycox_nll_p_kernel(
         for b in blocks:
             nc.vector.tensor_tensor(part[b][:], weighted_all[b][:, 0, :], e_case[b][:], ALU.add)
         for b in blocks:
-            nc.vector.tensor_tensor(den[b][:], weighted_all[b][:, 1, :], part[b][:], ALU.add)
+            for cases, entries in pieces(1 + b):
+                nc.vector.tensor_tensor(den[b][:, cases], weighted_all[b][:, 1, cases], part[b][:, cases], ALU.add)
 
         for b in blocks:
             log_den = fresh("log_den", b)
@@ -163,4 +173,5 @@ def tile_picked_ycox_nll_p_kernel(
             for cases, entries in pieces(2):
                 nc.scalar.activation(log_den[:, cases], den[b][:, cases], ACT.Ln)
                 nc.vector.tensor_tensor(result[:, cases], log_den[:, cases], top[b][:, cases], ALU.add)
-            nc.sync.dma_start(out=out[b * P : (b + 1) * P, :], in_=result)
+            for cases, entries in pieces(1 + b):
+                nc.sync.dma_start(out=out[b * P : (b + 1) * P, cases], in_=result[:, cases])

@@ -5,6 +5,8 @@ import concourse.mybir as mybir
 K, T, S, V, N, D = 512, 2048, 512, 256, 256, 2
 P = 128
 PACK = 4
+QUADRANT = 32
+LIST_ROWS = 16
 HALF = S // 2
 FLOPS = 2 * K * N * S
 
@@ -18,46 +20,60 @@ FP8X4 = mybir.dt.float8_e4m3fn_x4
 ALU = mybir.AluOpType
 ACT = mybir.ActivationFunctionType
 
+CODE_HALF_BYTES = 4 * HALF
+SCALE_TABLE_AT = 0
+X_CODES_AT = T
+W_BF0_AT = X_CODES_AT + CODE_HALF_BYTES // 2
+
+
+def pieces(count):
+    width = V // count
+    return [
+        (slice(i * width, (i + 1) * width), slice(i * width // LIST_ROWS, (i + 1) * width // LIST_ROWS))
+        for i in range(count)
+    ]
+
 
 def tile_picked_ycox_nll_p_kernel(
     tc, x_words, x_scales, w1, wgt, offs, case, pos1, pos2, out
 ):
     nc = tc.nc
     blocks = range(N // P)
+    first, last = blocks[0], blocks[-1]
     with ExitStack() as ctx:
         keep = ctx.enter_context(tc.tile_pool(name="keep", bufs=1))
         psum = ctx.enter_context(tc.psum_pool(name="psum", bufs=1))
         shared = ctx.enter_context(tc.tile_pool(name="shared", bufs=1))
 
-        scale_table = shared.tile([P, T], U8, name="scale_table", align_bytes=64, offset=0)
+        scale_table = shared.tile([P, T], U8, name="scale_table", align_bytes=64, offset=SCALE_TABLE_AT)
         nc.vector.memset(scale_table[:].bitcast(I32), 0)
         w_raw = [keep.tile([P, PACK, P], F32, name="w_raw%d" % b) for b in blocks]
 
         def load_w(b):
             nc.sync.dma_start(
-                out=w_raw[b][:], in_=w1[:, b * P : (b + 1) * P].rearrange("(p j) m -> p j m", j=PACK)
+                out=w_raw[b][:], in_=w1[:, b * P : (b + 1) * P].rearrange("(p t) m -> p t m", t=PACK)
             )
 
-        load_w(0)
-        offs_sb = keep.tile([P, S // 16], U16, name="offs_sb")
+        load_w(first)
+        offs_sb = keep.tile([P, S // LIST_ROWS], U16, name="offs_sb")
         nc.sync.dma_start(offs_sb[:], offs)
-        for q in range(4):
+        for q in range(P // QUADRANT):
             queue = nc.sync if q % 2 == 0 else nc.scalar
             queue.dma_start(
-                out=scale_table[32 * q : 32 * q + 4, :].bitcast(I32),
-                in_=x_scales[0, 4 * q : 4 * q + 4, :].bitcast(I32),
+                out=scale_table[QUADRANT * q : QUADRANT * q + PACK, :].bitcast(I32),
+                in_=x_scales[0, PACK * q : PACK * (q + 1), :].bitcast(I32),
             )
         word_table = keep.tile([P, T], U32, name="word_table", align_bytes=64)
         nc.sync.dma_start(
             out=word_table[:].bitcast(I32),
-            in_=x_words[0].rearrange("p c r -> p (c r)").bitcast(I32),
+            in_=x_words[0].rearrange("p c t -> p (c t)").bitcast(I32),
         )
-        load_w(1)
-        case_sb = keep.tile([P, V // 16], U16, name="case_sb")
+        load_w(last)
+        case_sb = keep.tile([P, V // LIST_ROWS], U16, name="case_sb")
         nc.sync.dma_start(case_sb[:], case)
         pos_sb = []
         for d, pos in enumerate((pos1, pos2)):
-            pos_d = keep.tile([P, V // 16], U16, name="pos_sb%d" % d)
+            pos_d = keep.tile([P, V // LIST_ROWS], U16, name="pos_sb%d" % d)
             nc.sync.dma_start(pos_d[:], pos)
             pos_sb.append(pos_d)
         wgt_sb = keep.tile([P, D, V], F32, name="wgt_sb")
@@ -67,36 +83,37 @@ def tile_picked_ycox_nll_p_kernel(
         nc.vector.tensor_copy(x_scale[:], scale_table[:].indirect(offs_sb[:]))
 
         w_bf = [
-            shared.tile([P, P, PACK], BF16, name="w_bf0", align_bytes=64, offset=2048 + 512),
+            shared.tile([P, P, PACK], BF16, name="w_bf0", align_bytes=64, offset=W_BF0_AT),
             keep.tile([P, P, PACK], BF16, name="w_bf1", align_bytes=64),
         ]
         w_code = [
-            shared.tile([P, P], U32, name="w_code0", align_bytes=64, offset=0),
+            shared.tile([P, P], U32, name="w_code0", align_bytes=64, offset=SCALE_TABLE_AT),
             keep.tile([P, P], U32, name="w_code1", align_bytes=64),
         ]
         w_scale = [keep.tile([P, P], U8, name="w_scale%d" % b, align_bytes=64) for b in blocks]
 
         def quantise_w(b):
-            nc.scalar.activation(w_bf[b][:], w_raw[b][:].rearrange("p j m -> p m j"), ACT.Copy)
+            nc.scalar.activation(w_bf[b][:], w_raw[b][:].rearrange("p t m -> p m t"), ACT.Copy)
             nc.vector.quantize_mx(
                 out=w_code[b][:].bitcast(FP8X4),
                 scales=w_scale[b][:],
-                in_=w_bf[b][:].rearrange("p m j -> p (m j)"),
+                in_=w_bf[b][:].rearrange("p m t -> p (m t)"),
             )
 
-        quantise_w(0)
+        quantise_w(first)
         x_code = []
-        for h in range(2):
-            code_h = shared.tile([P, HALF], U32, name="x_code%d" % h, align_bytes=64, offset=2048 + h * 1024)
-            nc.vector.tensor_copy(
-                code_h[:], word_table[:].indirect(offs_sb[:, h * HALF // 16 : (h + 1) * HALF // 16])
+        for h in range(S // HALF):
+            code_h = shared.tile(
+                [P, HALF], U32, name="x_code%d" % h, align_bytes=64, offset=X_CODES_AT + h * CODE_HALF_BYTES
             )
+            entries = slice(h * HALF // LIST_ROWS, (h + 1) * HALF // LIST_ROWS)
+            nc.vector.tensor_copy(code_h[:], word_table[:].indirect(offs_sb[:, entries]))
             x_code.append(code_h)
-        quantise_w(1)
+        quantise_w(last)
 
         y = [keep.tile([P, S], F32, name="y%d" % b) for b in blocks]
 
-        def product(b, h, start, width, on_vector=False):
+        def product(b, h, start, width):
             cols = slice(h * HALF + start, h * HALF + start + width)
             acc = psum.tile([P, width], F32, name="acc%d_%d" % (b, cols.start))
             nc.tensor.matmul_mx(
@@ -108,70 +125,60 @@ def tile_picked_ycox_nll_p_kernel(
                 start=True,
                 stop=True,
             )
-            if on_vector:
-                nc.vector.tensor_copy(y[b][:, cols], acc[:])
-            else:
-                nc.scalar.activation(y[b][:, cols], acc[:], ACT.Copy)
+            nc.scalar.activation(y[b][:, cols], acc[:], ACT.Copy)
 
-        product(0, 0, 0, HALF)
-        product(0, 1, 0, P)
-        product(0, 1, P, P, on_vector=True)
-        product(1, 0, 0, HALF)
-        product(1, 1, 0, HALF)
+        product(first, 0, 0, HALF)
+        product(first, 1, 0, HALF // 2)
+        product(first, 1, HALF // 2, HALF // 2)
+        product(last, 0, 0, HALF)
+        product(last, 1, 0, HALF)
 
-        def fresh(label, b):
+        def case_tile(label, b):
             return keep.tile([P, V], F32, name="%s%d" % (label, b))
 
-        def pieces(count):
-            width = V // count
-            return [
-                (slice(i * width, (i + 1) * width), slice(i * width // 16, (i + 1) * width // 16))
-                for i in range(count)
-            ]
 
         diff = []
         for b in blocks:
-            yc = fresh("yc", b)
-            for cases, entries in pieces(2 if b == 0 else 1):
+            yc = case_tile("yc", b)
+            for cases, entries in pieces(2 if b == first else 1):
                 nc.vector.tensor_copy(yc[:, cases], y[b][:].indirect(case_sb[:, entries]))
-            diff_b = [fresh("diff%d" % d, b) for d in range(D)]
+            diff_b = [case_tile("diff%d" % d, b) for d in range(D)]
             for d in range(D):
-                for cases, entries in pieces(2 if (b, d) == (0, 0) else 1):
+                for cases, entries in pieces(2 if (b, d) == (first, 0) else 1):
                     nc.vector.tensor_tensor(
                         diff_b[d][:, cases], y[b][:].indirect(pos_sb[d][:, entries]), yc[:, cases], ALU.subtract
                     )
             diff.append(diff_b)
 
-        top = [fresh("top", b) for b in blocks]
-        e_case = [fresh("e_case", b) for b in blocks]
+        top = [case_tile("top", b) for b in blocks]
+        e_case = [case_tile("e_case", b) for b in blocks]
         for b in blocks:
             nc.vector.scalar_tensor_tensor(top[b][:], diff[b][0][:], 0.0, diff[b][1][:], ALU.max, ALU.max)
             nc.scalar.activation(e_case[b][:], top[b][:], ACT.Exp, scale=-1.0)
 
-        e_ctl = [keep.tile([P, D, V], F32, name="e_ctl%d" % b) for b in blocks]
+        e_control = [keep.tile([P, D, V], F32, name="e_control%d" % b) for b in blocks]
         for b in blocks:
             for d in range(D):
-                shifted = fresh("shifted%d" % d, b)
-                for cases, entries in pieces(2 if (b, d) == (1, 1) else 1):
+                shifted = case_tile("shifted%d" % d, b)
+                for cases, entries in pieces(2 if (b, d) == (last, D - 1) else 1):
                     nc.vector.tensor_tensor(shifted[:, cases], diff[b][d][:, cases], top[b][:, cases], ALU.subtract)
-                    nc.scalar.activation(e_ctl[b][:, d, cases], shifted[:, cases], ACT.Exp)
+                    nc.scalar.activation(e_control[b][:, d, cases], shifted[:, cases], ACT.Exp)
 
-        weighted_all = [keep.tile([P, D, V], F32, name="weighted%d" % b) for b in blocks]
-        part = [fresh("part", b) for b in blocks]
-        den = [fresh("den", b) for b in blocks]
+        weighted = [keep.tile([P, D, V], F32, name="weighted%d" % b) for b in blocks]
+        part = [case_tile("part", b) for b in blocks]
+        den = [case_tile("den", b) for b in blocks]
         for b in blocks:
-            nc.vector.tensor_tensor(weighted_all[b][:], e_ctl[b][:], wgt_sb[:], ALU.mult)
+            nc.vector.tensor_tensor(weighted[b][:], e_control[b][:], wgt_sb[:], ALU.mult)
         for b in blocks:
-            nc.vector.tensor_tensor(part[b][:], weighted_all[b][:, 0, :], e_case[b][:], ALU.add)
+            nc.vector.tensor_tensor(part[b][:], weighted[b][:, 0, :], e_case[b][:], ALU.add)
         for b in blocks:
-            for cases, entries in pieces(1 + b):
-                nc.vector.tensor_tensor(den[b][:, cases], weighted_all[b][:, 1, cases], part[b][:, cases], ALU.add)
+            for cases, entries in pieces(2 if b == last else 1):
+                nc.vector.tensor_tensor(den[b][:, cases], weighted[b][:, 1, cases], part[b][:, cases], ALU.add)
 
         for b in blocks:
-            log_den = fresh("log_den", b)
-            result = weighted_all[-1][:, D - 1 - b, :]
+            log_den = case_tile("log_den", b)
+            result = e_case[last - b][:]
             for cases, entries in pieces(2):
                 nc.scalar.activation(log_den[:, cases], den[b][:, cases], ACT.Ln)
                 nc.vector.tensor_tensor(result[:, cases], log_den[:, cases], top[b][:, cases], ALU.add)
-            for cases, entries in pieces(1 + b):
-                nc.sync.dma_start(out=out[b * P : (b + 1) * P, cases], in_=result[:, cases])
+            nc.sync.dma_start(out=out[b * P : (b + 1) * P, :], in_=result)

@@ -68,16 +68,15 @@ def tile_picked_ycox_nll_p_kernel(
             out=word_table[:].bitcast(I32),
             in_=x_words[0].rearrange("p c t -> p (c t)").bitcast(I32),
         )
-        load_w(last)
-        case_sb = keep.tile([P, V // LIST_ROWS], U16, name="case_sb")
-        nc.sync.dma_start(case_sb[:], case)
-        pos_sb = []
-        for d, pos in enumerate((pos1, pos2)):
-            pos_d = keep.tile([P, V // LIST_ROWS], U16, name="pos_sb%d" % d)
-            nc.sync.dma_start(pos_d[:], pos)
-            pos_sb.append(pos_d)
         wgt_sb = keep.tile([P, D, V], F32, name="wgt_sb")
         nc.sync.dma_start(out=wgt_sb[:], in_=wgt.rearrange("d p v -> p d v"))
+        load_w(last)
+        pos2_sb = keep.tile([P, V // LIST_ROWS], U16, name="pos2_sb")
+        nc.sync.dma_start(pos2_sb[:], pos2)
+        pos1_sb = keep.tile([P, V // LIST_ROWS], U16, name="pos1_sb")
+        nc.sync.dma_start(pos1_sb[:], pos1)
+        case_sb = keep.tile([P, V // LIST_ROWS], U16, name="case_sb")
+        nc.sync.dma_start(case_sb[:], case)
 
         x_scale = keep.tile([P, S], U8, name="x_scale", align_bytes=64)
         nc.vector.tensor_copy(x_scale[:], scale_table[:].indirect(offs_sb[:]))
@@ -93,14 +92,19 @@ def tile_picked_ycox_nll_p_kernel(
         w_scale = [keep.tile([P, P], U8, name="w_scale%d" % b, align_bytes=64) for b in blocks]
 
         def quantise_w(b):
-            nc.scalar.activation(w_bf[b][:], w_raw[b][:].rearrange("p t m -> p m t"), ACT.Copy)
             nc.vector.quantize_mx(
                 out=w_code[b][:].bitcast(FP8X4),
                 scales=w_scale[b][:],
                 in_=w_bf[b][:].rearrange("p m t -> p (m t)"),
             )
 
+        def interleaved(b):
+            return w_raw[b][:].rearrange("p t m -> p m t")
+
+        nc.scalar.activation(w_bf[first][:], interleaved(first), ACT.Copy)
         quantise_w(first)
+        log_wgt = keep.tile([P, D, V], F32, name="log_wgt")
+        nc.scalar.activation(log_wgt[:], wgt_sb[:], ACT.Ln)
         x_code = []
         for h in range(S // HALF):
             code_h = shared.tile(
@@ -109,6 +113,9 @@ def tile_picked_ycox_nll_p_kernel(
             entries = slice(h * HALF // LIST_ROWS, (h + 1) * HALF // LIST_ROWS)
             nc.vector.tensor_copy(code_h[:], word_table[:].indirect(offs_sb[:, entries]))
             x_code.append(code_h)
+        nc.vector.tensor_copy(w_bf[last][:], interleaved(last))
+        log_ratio = keep.tile([P, V], F32, name="log_ratio")
+        nc.vector.tensor_tensor(log_ratio[:], log_wgt[:, 1, :], log_wgt[:, 0, :], ALU.subtract)
         quantise_w(last)
 
         y = [keep.tile([P, S], F32, name="y%d" % b) for b in blocks]
@@ -136,49 +143,61 @@ def tile_picked_ycox_nll_p_kernel(
         def case_tile(label, b):
             return keep.tile([P, V], F32, name="%s%d" % (label, b))
 
+        warm = keep.tile([P, 1], F32, name="warm")
+        nc.scalar.activation(warm[:], y[last][:, S - 1 : S], ACT.Exp, scale=0.0)
 
-        diff = []
-        for b in blocks:
-            yc = case_tile("yc", b)
-            for cases, entries in pieces(2 if b == first else 1):
-                nc.vector.tensor_copy(yc[:, cases], y[b][:].indirect(case_sb[:, entries]))
-            diff_b = [case_tile("diff%d" % d, b) for d in range(D)]
-            for d in range(D):
-                for cases, entries in pieces(2 if (b, d) == (first, 0) else 1):
-                    nc.vector.tensor_tensor(
-                        diff_b[d][:, cases], y[b][:].indirect(pos_sb[d][:, entries]), yc[:, cases], ALU.subtract
-                    )
-            diff.append(diff_b)
+        second = [case_tile("second", b) for b in blocks]
+        gap = [case_tile("gap", b) for b in blocks]
+        below = [case_tile("below", b) for b in blocks]
+        lead = [case_tile("lead", b) for b in blocks]
+        gap_abs = [case_tile("gap_abs", b) for b in blocks]
+        e_gap = [case_tile("e_gap", b) for b in blocks]
+        e_up = [case_tile("e_up", b) for b in blocks]
+        e_down = [case_tile("e_down", b) for b in blocks]
 
-        top = [case_tile("top", b) for b in blocks]
-        e_case = [case_tile("e_case", b) for b in blocks]
-        for b in blocks:
-            nc.vector.scalar_tensor_tensor(top[b][:], diff[b][0][:], 0.0, diff[b][1][:], ALU.max, ALU.max)
-            nc.scalar.activation(e_case[b][:], top[b][:], ACT.Exp, scale=-1.0)
+        def look_up(dst, b, offsets, other, op, count):
+            for cases, entries in pieces(count):
+                nc.vector.tensor_tensor(dst[:, cases], y[b][:].indirect(offsets[:, entries]), other[:, cases], op)
 
-        e_control = [keep.tile([P, D, V], F32, name="e_control%d" % b) for b in blocks]
-        for b in blocks:
-            for d in range(D):
-                shifted = case_tile("shifted%d" % d, b)
-                for cases, entries in pieces(2 if (b, d) == (last, D - 1) else 1):
-                    nc.vector.tensor_tensor(shifted[:, cases], diff[b][d][:, cases], top[b][:, cases], ALU.subtract)
-                    nc.scalar.activation(e_control[b][:, d, cases], shifted[:, cases], ACT.Exp)
+        def gap_exp(b):
+            nc.scalar.activation(gap_abs[b][:], gap[b][:], ACT.Abs)
+            nc.scalar.activation(e_gap[b][:], gap_abs[b][:], ACT.Exp, scale=-1.0)
 
-        weighted = [keep.tile([P, D, V], F32, name="weighted%d" % b) for b in blocks]
-        part = [case_tile("part", b) for b in blocks]
+        def lead_exp(b, count):
+            for cases, entries in pieces(count):
+                nc.vector.scalar_tensor_tensor(
+                    lead[b][:, cases], gap[b][:, cases], 0.0, below[b][:, cases], ALU.max, ALU.subtract
+                )
+                nc.scalar.activation(e_up[b][:, cases], lead[b][:, cases], ACT.Exp)
+                nc.scalar.activation(e_down[b][:, cases], lead[b][:, cases], ACT.Exp, scale=-1.0)
+
+        look_up(second[first], first, pos2_sb, log_ratio, ALU.add, 2)
+        look_up(gap[first], first, pos1_sb, second[first], ALU.subtract, 2)
+        gap_exp(first)
+        look_up(below[first], first, case_sb, second[first], ALU.subtract, 1)
+        look_up(second[last], last, pos2_sb, log_ratio, ALU.add, 1)
+        lead_exp(first, 1)
+        look_up(gap[last], last, pos1_sb, second[last], ALU.subtract, 1)
+        gap_exp(last)
+        look_up(below[last], last, case_sb, second[last], ALU.subtract, 2)
+        lead_exp(last, 2)
+
+        pair = [case_tile("pair", b) for b in blocks]
+        controls = [case_tile("controls", b) for b in blocks]
         den = [case_tile("den", b) for b in blocks]
         for b in blocks:
-            nc.vector.tensor_tensor(weighted[b][:], e_control[b][:], wgt_sb[:], ALU.mult)
+            nc.vector.scalar_tensor_tensor(pair[b][:], e_gap[b][:], 1.0, wgt_sb[:, 0, :], ALU.add, ALU.mult)
         for b in blocks:
-            nc.vector.tensor_tensor(part[b][:], weighted[b][:, 0, :], e_case[b][:], ALU.add)
+            nc.vector.scalar_tensor_tensor(controls[b][:], e_up[b][:], 1.0, pair[b][:], ALU.min, ALU.mult)
         for b in blocks:
-            for cases, entries in pieces(2 if b == last else 1):
-                nc.vector.tensor_tensor(den[b][:, cases], weighted[b][:, 1, cases], part[b][:, cases], ALU.add)
+            nc.vector.scalar_tensor_tensor(den[b][:], e_down[b][:], 1.0, controls[b][:], ALU.min, ALU.add)
 
         for b in blocks:
             log_den = case_tile("log_den", b)
-            result = e_case[last - b][:]
+            result = e_down[last - b][:]
             for cases, entries in pieces(2):
                 nc.scalar.activation(log_den[:, cases], den[b][:, cases], ACT.Ln)
-                nc.vector.tensor_tensor(result[:, cases], log_den[:, cases], top[b][:, cases], ALU.add)
+                nc.vector.scalar_tensor_tensor(
+                    result[:, cases], lead[b][:, cases], 0.0, log_den[:, cases], ALU.max, ALU.add
+                )
             nc.sync.dma_start(out=out[b * P : (b + 1) * P, :], in_=result)

@@ -1,6 +1,7 @@
 from contextlib import ExitStack
 
 import concourse.mybir as mybir
+from concourse.masks import make_identity
 
 K, T, S, V, N, D = 512, 2048, 512, 256, 256, 2
 P = 128
@@ -8,6 +9,8 @@ PACK = 4
 QUADRANT = 32
 LIST_ROWS = 16
 HALF = S // 2
+BANK_BYTES = 2048
+PRODUCT_BANKS = 5
 FLOPS = 2 * K * N * S
 
 F32 = mybir.dt.float32
@@ -63,13 +66,17 @@ def tile_picked_ycox_nll_p_kernel(
                 out=scale_table[QUADRANT * q : QUADRANT * q + PACK, :].bitcast(I32),
                 in_=x_scales[0, PACK * q : PACK * (q + 1), :].bitcast(I32),
             )
+        wgt_rows = keep.tile([P, V], F32, name="wgt_rows")
+        nc.vector.memset(wgt_rows[:], 0.0)
+        nc.sync.dma_start(out=wgt_rows[:D, :], in_=wgt[:, 0, :])
+        identity = keep.tile([P, P], F32, name="identity")
+        nc.vector.memset(identity[:], 0.0)
+        make_identity(nc, identity[:], nomemset=True)
         word_table = keep.tile([P, T], U32, name="word_table", align_bytes=64)
         nc.sync.dma_start(
             out=word_table[:].bitcast(I32),
             in_=x_words[0].rearrange("p c t -> p (c t)").bitcast(I32),
         )
-        wgt_sb = keep.tile([P, D, V], F32, name="wgt_sb")
-        nc.sync.dma_start(out=wgt_sb[:], in_=wgt.rearrange("d p v -> p d v"))
         load_w(last)
         pos2_sb = keep.tile([P, V // LIST_ROWS], U16, name="pos2_sb")
         nc.sync.dma_start(pos2_sb[:], pos2)
@@ -77,13 +84,14 @@ def tile_picked_ycox_nll_p_kernel(
         nc.sync.dma_start(pos1_sb[:], pos1)
         case_sb = keep.tile([P, V // LIST_ROWS], U16, name="case_sb")
         nc.sync.dma_start(case_sb[:], case)
+        wgt0 = keep.tile([P, V], F32, name="wgt0")
+        nc.sync.dma_start(out=wgt0[:], in_=wgt[0])
 
         x_scale = keep.tile([P, S], U8, name="x_scale", align_bytes=64)
         nc.vector.tensor_copy(x_scale[:], scale_table[:].indirect(offs_sb[:]))
 
         w_bf = [
             shared.tile([P, P, PACK], BF16, name="w_bf0", align_bytes=64, offset=W_BF0_AT),
-            keep.tile([P, P, PACK], BF16, name="w_bf1", align_bytes=64),
         ]
         w_code = [
             shared.tile([P, P], U32, name="w_code0", align_bytes=64, offset=SCALE_TABLE_AT),
@@ -101,10 +109,33 @@ def tile_picked_ycox_nll_p_kernel(
         def interleaved(b):
             return w_raw[b][:].rearrange("p t m -> p m t")
 
+        one = keep.tile([P, 1], F32, name="one")
+        nc.vector.memset(one[:], 1.0)
+        warm_ln = keep.tile([P, 1], F32, name="warm_ln")
+        nc.scalar.activation(warm_ln[:], one[:], ACT.Ln)
         nc.scalar.activation(w_bf[first][:], interleaved(first), ACT.Copy)
         quantise_w(first)
-        log_wgt = keep.tile([P, D, V], F32, name="log_wgt")
-        nc.scalar.activation(log_wgt[:], wgt_sb[:], ACT.Ln)
+
+        halves = V // P
+        wgt_cols = psum.tile([P, halves, P], F32, name="wgt_cols", offset=PRODUCT_BANKS * BANK_BYTES)
+        for h in range(halves):
+            nc.tensor.transpose(wgt_cols[:, h, :], wgt_rows[:, h * P : (h + 1) * P], identity[:])
+        log_cols = keep.tile([P, halves, D], F32, name="log_cols")
+        nc.scalar.activation(log_cols[:], wgt_cols[:, :, :D], ACT.Ln)
+        ratio_cols = keep.tile([P, halves], F32, name="ratio_cols", tag="w_bf1", align_bytes=64)
+        for h in range(halves):
+            nc.scalar.activation(
+                ratio_cols[:, h : h + 1], log_cols[:, h, 0:1], ACT.Identity, scale=-1.0, bias=log_cols[:, h, 1:2]
+            )
+        ratio_ps = psum.tile([P, PRODUCT_BANKS * BANK_BYTES // 4], F32, name="ratio_ps", offset=0)
+        for h in range(halves):
+            nc.tensor.transpose(
+                ratio_ps[:, h * P : (h + 1) * P], ratio_cols[:, h : h + 1].to_broadcast([P, P]), identity[:]
+            )
+        log_ratio = keep.tile([P, V], F32, name="log_ratio")
+        nc.scalar.activation(log_ratio[:], ratio_ps[:, :V], ACT.Copy)
+        w_bf.append(keep.tile([P, P, PACK], BF16, name="w_bf1", align_bytes=64))
+
         x_code = []
         for h in range(S // HALF):
             code_h = shared.tile(
@@ -113,16 +144,14 @@ def tile_picked_ycox_nll_p_kernel(
             entries = slice(h * HALF // LIST_ROWS, (h + 1) * HALF // LIST_ROWS)
             nc.vector.tensor_copy(code_h[:], word_table[:].indirect(offs_sb[:, entries]))
             x_code.append(code_h)
-        nc.vector.tensor_copy(w_bf[last][:], interleaved(last))
-        log_ratio = keep.tile([P, V], F32, name="log_ratio")
-        nc.vector.tensor_tensor(log_ratio[:], log_wgt[:, 1, :], log_wgt[:, 0, :], ALU.subtract)
+        nc.scalar.activation(w_bf[last][:], interleaved(last), ACT.Copy)
         quantise_w(last)
 
         y = [keep.tile([P, S], F32, name="y%d" % b) for b in blocks]
 
-        def product(b, h, start, width):
+        def product(bank, b, h, start, width):
             cols = slice(h * HALF + start, h * HALF + start + width)
-            acc = psum.tile([P, width], F32, name="acc%d_%d" % (b, cols.start))
+            acc = psum.tile([P, width], F32, name="acc%d" % bank, offset=bank * BANK_BYTES)
             nc.tensor.matmul_mx(
                 out=acc[:],
                 lhsT=w_code[b][:].bitcast(FP8X4),
@@ -134,11 +163,11 @@ def tile_picked_ycox_nll_p_kernel(
             )
             nc.scalar.activation(y[b][:, cols], acc[:], ACT.Copy)
 
-        product(first, 0, 0, HALF)
-        product(first, 1, 0, HALF // 2)
-        product(first, 1, HALF // 2, HALF // 2)
-        product(last, 0, 0, HALF)
-        product(last, 1, 0, HALF)
+        product(0, first, 0, 0, HALF)
+        product(1, first, 1, 0, HALF // 2)
+        product(2, first, 1, HALF // 2, HALF // 2)
+        product(3, last, 0, 0, HALF)
+        product(4, last, 1, 0, HALF)
 
         def case_tile(label, b):
             return keep.tile([P, V], F32, name="%s%d" % (label, b))
@@ -155,38 +184,47 @@ def tile_picked_ycox_nll_p_kernel(
         e_up = [case_tile("e_up", b) for b in blocks]
         e_down = [case_tile("e_down", b) for b in blocks]
 
-        def look_up(dst, b, offsets, other, op, count):
-            for cases, entries in pieces(count):
-                nc.vector.tensor_tensor(dst[:, cases], y[b][:].indirect(offsets[:, entries]), other[:, cases], op)
+        def look_up(dst, b, offsets, other, op, piece):
+            cases, entries = piece
+            nc.vector.tensor_tensor(dst[:, cases], y[b][:].indirect(offsets[:, entries]), other[:, cases], op)
 
-        def gap_exp(b):
-            nc.scalar.activation(gap_abs[b][:], gap[b][:], ACT.Abs)
-            nc.scalar.activation(e_gap[b][:], gap_abs[b][:], ACT.Exp, scale=-1.0)
+        def gap_exp(b, piece):
+            cases, entries = piece
+            nc.scalar.activation(gap_abs[b][:, cases], gap[b][:, cases], ACT.Abs)
+            nc.scalar.activation(e_gap[b][:, cases], gap_abs[b][:, cases], ACT.Exp, scale=-1.0)
 
-        def lead_exp(b, count):
-            for cases, entries in pieces(count):
-                nc.vector.scalar_tensor_tensor(
-                    lead[b][:, cases], gap[b][:, cases], 0.0, below[b][:, cases], ALU.max, ALU.subtract
-                )
-                nc.scalar.activation(e_up[b][:, cases], lead[b][:, cases], ACT.Exp)
-                nc.scalar.activation(e_down[b][:, cases], lead[b][:, cases], ACT.Exp, scale=-1.0)
+        def lead_exp(b, piece):
+            cases, entries = piece
+            nc.vector.scalar_tensor_tensor(
+                lead[b][:, cases], gap[b][:, cases], 0.0, below[b][:, cases], ALU.max, ALU.subtract
+            )
+            nc.scalar.activation(e_up[b][:, cases], lead[b][:, cases], ACT.Exp)
+            nc.scalar.activation(e_down[b][:, cases], lead[b][:, cases], ACT.Exp, scale=-1.0)
 
-        look_up(second[first], first, pos2_sb, log_ratio, ALU.add, 2)
-        look_up(gap[first], first, pos1_sb, second[first], ALU.subtract, 2)
-        gap_exp(first)
-        look_up(below[first], first, case_sb, second[first], ALU.subtract, 1)
-        look_up(second[last], last, pos2_sb, log_ratio, ALU.add, 1)
-        lead_exp(first, 1)
-        look_up(gap[last], last, pos1_sb, second[last], ALU.subtract, 1)
-        gap_exp(last)
-        look_up(below[last], last, case_sb, second[last], ALU.subtract, 2)
-        lead_exp(last, 2)
+        (whole,) = pieces(1)
+        low, high = pieces(2)
+        for piece in (low, high):
+            look_up(second[first], first, pos2_sb, log_ratio, ALU.add, piece)
+        for piece in (low, high):
+            look_up(gap[first], first, pos1_sb, second[first], ALU.subtract, piece)
+        gap_exp(first, whole)
+        look_up(below[first], first, case_sb, second[first], ALU.subtract, whole)
+        look_up(second[last], last, pos2_sb, log_ratio, ALU.add, whole)
+        lead_exp(first, whole)
+        look_up(gap[last], last, pos1_sb, second[last], ALU.subtract, low)
+        gap_exp(last, low)
+        look_up(below[last], last, case_sb, second[last], ALU.subtract, low)
+        look_up(gap[last], last, pos1_sb, second[last], ALU.subtract, high)
+        gap_exp(last, high)
+        lead_exp(last, low)
+        look_up(below[last], last, case_sb, second[last], ALU.subtract, high)
+        lead_exp(last, high)
 
-        pair = [case_tile("pair", b) for b in blocks]
+        pair = [gap[last], below[last]]
         controls = [case_tile("controls", b) for b in blocks]
         den = [case_tile("den", b) for b in blocks]
         for b in blocks:
-            nc.vector.scalar_tensor_tensor(pair[b][:], e_gap[b][:], 1.0, wgt_sb[:, 0, :], ALU.add, ALU.mult)
+            nc.vector.scalar_tensor_tensor(pair[b][:], e_gap[b][:], 1.0, wgt0[:], ALU.add, ALU.mult)
         for b in blocks:
             nc.vector.scalar_tensor_tensor(controls[b][:], e_up[b][:], 1.0, pair[b][:], ALU.min, ALU.mult)
         for b in blocks:

@@ -1,3 +1,4 @@
+import math
 from contextlib import ExitStack
 
 import concourse.mybir as mybir
@@ -11,6 +12,7 @@ LIST_ROWS = 16
 HALF = S // 2
 BANK_BYTES = 2048
 PRODUCT_BANKS = 5
+LEAD_CAP = 30.0
 FLOPS = 2 * K * N * S
 
 F32 = mybir.dt.float32
@@ -177,65 +179,61 @@ def tile_picked_ycox_nll_p_kernel(
 
         second = [case_tile("second", b) for b in blocks]
         gap = [case_tile("gap", b) for b in blocks]
-        below = [case_tile("below", b) for b in blocks]
-        lead = [case_tile("lead", b) for b in blocks]
+        larger = [case_tile("larger", b) for b in blocks]
+        lag = [case_tile("lag", b) for b in blocks]
         gap_abs = [case_tile("gap_abs", b) for b in blocks]
         e_gap = [case_tile("e_gap", b) for b in blocks]
-        e_up = [case_tile("e_up", b) for b in blocks]
-        e_down = [case_tile("e_down", b) for b in blocks]
+        e_lead = [case_tile("e_lead", b) for b in blocks]
 
-        def look_up(dst, b, offsets, other, op, piece):
-            cases, entries = piece
-            nc.vector.tensor_tensor(dst[:, cases], y[b][:].indirect(offsets[:, entries]), other[:, cases], op)
+        def look_up(dst, b, offsets, other, op, count):
+            for cases, entries in pieces(count):
+                nc.vector.tensor_tensor(dst[:, cases], y[b][:].indirect(offsets[:, entries]), other[:, cases], op)
 
-        def gap_exp(b, piece):
-            cases, entries = piece
-            nc.scalar.activation(gap_abs[b][:, cases], gap[b][:, cases], ACT.Abs)
-            nc.scalar.activation(e_gap[b][:, cases], gap_abs[b][:, cases], ACT.Exp, scale=-1.0)
+        def look_up_second(b, count):
+            look_up(second[b], b, pos2_sb, log_ratio, ALU.add, count)
 
-        def lead_exp(b, piece):
-            cases, entries = piece
-            nc.vector.scalar_tensor_tensor(
-                lead[b][:, cases], gap[b][:, cases], 0.0, below[b][:, cases], ALU.max, ALU.subtract
-            )
-            nc.scalar.activation(e_up[b][:, cases], lead[b][:, cases], ACT.Exp)
-            nc.scalar.activation(e_down[b][:, cases], lead[b][:, cases], ACT.Exp, scale=-1.0)
+        def look_up_gap(b, count):
+            look_up(gap[b], b, pos1_sb, second[b], ALU.subtract, count)
+            nc.scalar.activation(gap_abs[b][:], gap[b][:], ACT.Abs)
+            nc.scalar.activation(e_gap[b][:], gap_abs[b][:], ACT.Exp, scale=-1.0)
 
-        (whole,) = pieces(1)
-        low, high = pieces(2)
-        for piece in (low, high):
-            look_up(second[first], first, pos2_sb, log_ratio, ALU.add, piece)
-        for piece in (low, high):
-            look_up(gap[first], first, pos1_sb, second[first], ALU.subtract, piece)
-        gap_exp(first, whole)
-        look_up(below[first], first, case_sb, second[first], ALU.subtract, whole)
-        look_up(second[last], last, pos2_sb, log_ratio, ALU.add, whole)
-        lead_exp(first, whole)
-        look_up(gap[last], last, pos1_sb, second[last], ALU.subtract, low)
-        gap_exp(last, low)
-        look_up(below[last], last, case_sb, second[last], ALU.subtract, low)
-        look_up(gap[last], last, pos1_sb, second[last], ALU.subtract, high)
-        gap_exp(last, high)
-        lead_exp(last, low)
-        look_up(below[last], last, case_sb, second[last], ALU.subtract, high)
-        lead_exp(last, high)
-
-        pair = [gap[last], below[last]]
-        controls = [case_tile("controls", b) for b in blocks]
-        den = [case_tile("den", b) for b in blocks]
-        for b in blocks:
-            nc.vector.scalar_tensor_tensor(pair[b][:], e_gap[b][:], 1.0, wgt0[:], ALU.add, ALU.mult)
-        for b in blocks:
-            nc.vector.scalar_tensor_tensor(controls[b][:], e_up[b][:], 1.0, pair[b][:], ALU.min, ALU.mult)
-        for b in blocks:
-            nc.vector.scalar_tensor_tensor(den[b][:], e_down[b][:], 1.0, controls[b][:], ALU.min, ALU.add)
-
-        for b in blocks:
-            log_den = case_tile("log_den", b)
-            result = e_down[last - b][:]
-            for cases, entries in pieces(2):
-                nc.scalar.activation(log_den[:, cases], den[b][:, cases], ACT.Ln)
+        def take_larger(b, count):
+            for cases, entries in pieces(count):
                 nc.vector.scalar_tensor_tensor(
-                    result[:, cases], lead[b][:, cases], 0.0, log_den[:, cases], ALU.max, ALU.add
+                    larger[b][:, cases], gap[b][:, cases], 0.0, second[b][:, cases], ALU.max, ALU.add
                 )
+
+        def look_up_lag(b, count):
+            for cases, entries in pieces(count):
+                nc.vector.tensor_tensor(
+                    lag[b][:, cases], y[b][:].indirect(case_sb[:, entries]), larger[b][:, cases], ALU.subtract
+                )
+                nc.scalar.activation(e_lead[b][:, cases], lag[b][:, cases], ACT.Exp, scale=-1.0)
+
+        look_up_second(first, 2)
+        look_up_gap(first, 2)
+        look_up_second(last, 1)
+        take_larger(first, 1)
+        look_up_gap(last, 1)
+        look_up_lag(first, 1)
+        take_larger(last, 2)
+        look_up_lag(last, 2)
+
+        pair = [y[last][:, b * V : (b + 1) * V] for b in blocks]
+        controls = [case_tile("controls", b) for b in blocks]
+        for b in blocks:
+            nc.vector.scalar_tensor_tensor(pair[b], e_gap[b][:], 1.0, wgt0[:], ALU.add, ALU.mult)
+        for b in blocks:
+            nc.vector.scalar_tensor_tensor(
+                controls[b][:], e_lead[b][:], math.exp(LEAD_CAP), pair[b], ALU.min, ALU.mult
+            )
+        for b in blocks:
+            nc.vector.tensor_scalar(pair[b], lag[b][:], LEAD_CAP, 0.0, ALU.add, ALU.min)
+
+        for b in blocks:
+            log_sum = case_tile("log_sum", b)
+            result = lag[last - b][:]
+            for cases, entries in pieces(2):
+                nc.scalar.activation(log_sum[:, cases], controls[b][:, cases], ACT.Ln, bias=1.0)
+                nc.vector.tensor_tensor(result[:, cases], log_sum[:, cases], pair[b][:, cases], ALU.subtract)
             nc.sync.dma_start(out=out[b * P : (b + 1) * P, :], in_=result)

@@ -27,8 +27,8 @@ ACT = mybir.ActivationFunctionType
 
 CODE_HALF_BYTES = 4 * HALF
 SCALE_TABLE_AT = 0
-X_CODES_AT = T
-W_BF0_AT = X_CODES_AT + CODE_HALF_BYTES // 2
+X_CODES_AT = 0
+W_BF0_AT = T
 
 
 def pieces(count):
@@ -89,14 +89,11 @@ def tile_picked_ycox_nll_p_kernel(
         wgt0 = keep.tile([P, V], F32, name="wgt0")
         nc.sync.dma_start(out=wgt0[:], in_=wgt[0])
 
-        x_scale = keep.tile([P, S], U8, name="x_scale", align_bytes=64)
-        nc.vector.tensor_copy(x_scale[:], scale_table[:].indirect(offs_sb[:]))
-
         w_bf = [
             shared.tile([P, P, PACK], BF16, name="w_bf0", align_bytes=64, offset=W_BF0_AT),
         ]
         w_code = [
-            shared.tile([P, P], U32, name="w_code0", align_bytes=64, offset=SCALE_TABLE_AT),
+            keep.tile([P, P], U32, name="w_code0", align_bytes=64),
             keep.tile([P, P], U32, name="w_code1", align_bytes=64),
         ]
         w_scale = [keep.tile([P, P], U8, name="w_scale%d" % b, align_bytes=64) for b in blocks]
@@ -108,15 +105,22 @@ def tile_picked_ycox_nll_p_kernel(
                 in_=w_bf[b][:].rearrange("p m t -> p (m t)"),
             )
 
-        def interleaved(b):
-            return w_raw[b][:].rearrange("p t m -> p m t")
+        def cast_w(b):
+            nc.scalar.activation(
+                w_bf[b][:].rearrange("p (c i) t -> p c t i", i=PACK),
+                w_raw[b][:].rearrange("p t (c i) -> p c t i", i=PACK),
+                ACT.Copy,
+            )
 
         one = keep.tile([P, 1], F32, name="one")
         nc.vector.memset(one[:], 1.0)
         warm_ln = keep.tile([P, 1], F32, name="warm_ln")
         nc.scalar.activation(warm_ln[:], one[:], ACT.Ln)
-        nc.scalar.activation(w_bf[first][:], interleaved(first), ACT.Copy)
+        cast_w(first)
         quantise_w(first)
+        x_scale = shared.tile([P, S], U8, name="x_scale", align_bytes=64, offset=W_BF0_AT)
+        nc.vector.tensor_copy(x_scale[:], scale_table[:].indirect(offs_sb[:]))
+
 
         halves = V // P
         wgt_cols = psum.tile([P, halves, P], F32, name="wgt_cols", offset=PRODUCT_BANKS * BANK_BYTES)
@@ -146,7 +150,7 @@ def tile_picked_ycox_nll_p_kernel(
             entries = slice(h * HALF // LIST_ROWS, (h + 1) * HALF // LIST_ROWS)
             nc.vector.tensor_copy(code_h[:], word_table[:].indirect(offs_sb[:, entries]))
             x_code.append(code_h)
-        nc.scalar.activation(w_bf[last][:], interleaved(last), ACT.Copy)
+        cast_w(last)
         quantise_w(last)
 
         y = [keep.tile([P, S], F32, name="y%d" % b) for b in blocks]

@@ -10,9 +10,11 @@ PACK = 4
 QUADRANT = 32
 LIST_ROWS = 16
 HALF = S // 2
+CASE_TILES = V // P
+LINE_COLUMNS = 4
 BANK_BYTES = 2048
 PRODUCT_BANKS = 5
-LEAD_CAP = 30.0
+EXPONENT_CAP = 30.0
 FLOPS = 2 * K * N * S
 
 F32 = mybir.dt.float32
@@ -25,9 +27,8 @@ FP8X4 = mybir.dt.float8_e4m3fn_x4
 ALU = mybir.AluOpType
 ACT = mybir.ActivationFunctionType
 
-CODE_HALF_BYTES = 4 * HALF
 SCALE_TABLE_AT = 0
-X_CODES_AT = 0
+CODE_HALF_BYTES = 4 * HALF
 W_BF0_AT = T
 
 
@@ -89,69 +90,58 @@ def tile_picked_ycox_nll_p_kernel(
         wgt0 = keep.tile([P, V], F32, name="wgt0")
         nc.sync.dma_start(out=wgt0[:], in_=wgt[0])
 
-        w_bf = [
-            shared.tile([P, P, PACK], BF16, name="w_bf0", align_bytes=64, offset=W_BF0_AT),
-        ]
-        w_code = [
-            keep.tile([P, P], U32, name="w_code0", align_bytes=64),
-            keep.tile([P, P], U32, name="w_code1", align_bytes=64),
-        ]
+        w_code = [keep.tile([P, P], U32, name="w_code%d" % b, align_bytes=64) for b in blocks]
         w_scale = [keep.tile([P, P], U8, name="w_scale%d" % b, align_bytes=64) for b in blocks]
 
-        def quantise_w(b):
+        def cast_views(w_bf, b):
+            return (
+                w_bf[:].rearrange("p (c i) t -> p c t i", i=LINE_COLUMNS),
+                w_raw[b][:].rearrange("p t (c i) -> p c t i", i=LINE_COLUMNS),
+            )
+
+        def quantise_w(w_bf, b):
             nc.vector.quantize_mx(
                 out=w_code[b][:].bitcast(FP8X4),
                 scales=w_scale[b][:],
-                in_=w_bf[b][:].rearrange("p m t -> p (m t)"),
+                in_=w_bf[:].rearrange("p m t -> p (m t)"),
             )
 
-        def cast_w(b):
-            nc.scalar.activation(
-                w_bf[b][:].rearrange("p (c i) t -> p c t i", i=PACK),
-                w_raw[b][:].rearrange("p t (c i) -> p c t i", i=PACK),
-                ACT.Copy,
-            )
-
-        one = keep.tile([P, 1], F32, name="one")
-        nc.vector.memset(one[:], 1.0)
-        warm_ln = keep.tile([P, 1], F32, name="warm_ln")
-        nc.scalar.activation(warm_ln[:], one[:], ACT.Ln)
-        cast_w(first)
-        quantise_w(first)
+        w_bf0 = shared.tile([P, P, PACK], BF16, name="w_bf0", align_bytes=64, offset=W_BF0_AT)
+        nc.vector.tensor_copy(*cast_views(w_bf0, first))
+        quantise_w(w_bf0, first)
         x_scale = shared.tile([P, S], U8, name="x_scale", align_bytes=64, offset=W_BF0_AT)
         nc.vector.tensor_copy(x_scale[:], scale_table[:].indirect(offs_sb[:]))
 
-
-        halves = V // P
-        wgt_cols = psum.tile([P, halves, P], F32, name="wgt_cols", offset=PRODUCT_BANKS * BANK_BYTES)
-        for h in range(halves):
-            nc.tensor.transpose(wgt_cols[:, h, :], wgt_rows[:, h * P : (h + 1) * P], identity[:])
-        log_cols = keep.tile([P, halves, D], F32, name="log_cols")
+        wgt_cols = psum.tile([P, CASE_TILES, P], F32, name="wgt_cols", offset=PRODUCT_BANKS * BANK_BYTES)
+        for c in range(CASE_TILES):
+            nc.tensor.transpose(wgt_cols[:, c, :], wgt_rows[:, c * P : (c + 1) * P], identity[:])
+        log_cols = keep.tile([P, CASE_TILES, D], F32, name="log_cols")
         nc.scalar.activation(log_cols[:], wgt_cols[:, :, :D], ACT.Ln)
-        ratio_cols = keep.tile([P, halves], F32, name="ratio_cols", tag="w_bf1", align_bytes=64)
-        for h in range(halves):
+        ratio_cols = keep.tile([P, CASE_TILES], F32, name="ratio_cols", tag="w_bf1", align_bytes=64)
+        for c in range(CASE_TILES):
             nc.scalar.activation(
-                ratio_cols[:, h : h + 1], log_cols[:, h, 0:1], ACT.Identity, scale=-1.0, bias=log_cols[:, h, 1:2]
+                ratio_cols[:, c : c + 1], log_cols[:, c, 0:1], ACT.Identity, scale=-1.0, bias=log_cols[:, c, 1:2]
             )
-        ratio_ps = psum.tile([P, PRODUCT_BANKS * BANK_BYTES // 4], F32, name="ratio_ps", offset=0)
-        for h in range(halves):
+        ratio_banks = psum.tile([P, PRODUCT_BANKS * BANK_BYTES // 4], F32, name="ratio_banks", offset=0)
+        for c in range(CASE_TILES):
             nc.tensor.transpose(
-                ratio_ps[:, h * P : (h + 1) * P], ratio_cols[:, h : h + 1].to_broadcast([P, P]), identity[:]
+                ratio_banks[:, c * P : (c + 1) * P], ratio_cols[:, c : c + 1].to_broadcast([P, P]), identity[:]
             )
         log_ratio = keep.tile([P, V], F32, name="log_ratio")
-        nc.scalar.activation(log_ratio[:], ratio_ps[:, :V], ACT.Copy)
-        w_bf.append(keep.tile([P, P, PACK], BF16, name="w_bf1", align_bytes=64))
+        nc.scalar.activation(log_ratio[:], ratio_banks[:, :V], ACT.Copy)
 
         x_code = []
         for h in range(S // HALF):
             code_h = shared.tile(
-                [P, HALF], U32, name="x_code%d" % h, align_bytes=64, offset=X_CODES_AT + h * CODE_HALF_BYTES
+                [P, HALF], U32, name="x_code%d" % h, align_bytes=64, offset=SCALE_TABLE_AT + h * CODE_HALF_BYTES
             )
             entries = slice(h * HALF // LIST_ROWS, (h + 1) * HALF // LIST_ROWS)
             nc.vector.tensor_copy(code_h[:], word_table[:].indirect(offs_sb[:, entries]))
             x_code.append(code_h)
-        cast_w(last)
-        quantise_w(last)
+
+        w_bf1 = keep.tile([P, P, PACK], BF16, name="w_bf1", align_bytes=64)
+        nc.scalar.activation(*cast_views(w_bf1, last), ACT.Copy)
+        quantise_w(w_bf1, last)
 
         y = [keep.tile([P, S], F32, name="y%d" % b) for b in blocks]
 
@@ -169,37 +159,36 @@ def tile_picked_ycox_nll_p_kernel(
             )
             nc.scalar.activation(y[b][:, cols], acc[:], ACT.Copy)
 
-        product(0, first, 0, 0, HALF)
-        product(1, first, 1, 0, HALF // 2)
-        product(2, first, 1, HALF // 2, HALF // 2)
-        product(3, last, 0, 0, HALF)
-        product(4, last, 1, 0, HALF)
+        passes = [
+            (first, 0, 0, HALF),
+            (first, 1, 0, HALF // 2),
+            (first, 1, HALF // 2, HALF // 2),
+            (last, 0, 0, HALF),
+            (last, 1, 0, HALF),
+        ]
+        for bank, one_pass in enumerate(passes):
+            product(bank, *one_pass)
 
-        def case_tile(label, b):
-            return keep.tile([P, V], F32, name="%s%d" % (label, b))
+        def case_tile(label):
+            return keep.tile([P, V], F32, name=label)
 
-        warm = keep.tile([P, 1], F32, name="warm")
-        nc.scalar.activation(warm[:], y[last][:, S - 1 : S], ACT.Exp, scale=0.0)
+        second = [case_tile("second%d" % b) for b in blocks]
+        gap = [case_tile("gap%d" % b) for b in blocks]
+        larger = [case_tile("larger%d" % b) for b in blocks]
+        lag = [case_tile("lag%d" % b) for b in blocks]
+        exp_minus_lag = [case_tile("exp_minus_lag%d" % b) for b in blocks]
 
-        second = [case_tile("second", b) for b in blocks]
-        gap = [case_tile("gap", b) for b in blocks]
-        larger = [case_tile("larger", b) for b in blocks]
-        lag = [case_tile("lag", b) for b in blocks]
-        gap_abs = [case_tile("gap_abs", b) for b in blocks]
-        e_gap = [case_tile("e_gap", b) for b in blocks]
-        e_lead = [case_tile("e_lead", b) for b in blocks]
-
-        def look_up(dst, b, offsets, other, op, count):
-            for cases, entries in pieces(count):
-                nc.vector.tensor_tensor(dst[:, cases], y[b][:].indirect(offsets[:, entries]), other[:, cases], op)
+        def look_up(dst, b, offsets, other, op, piece):
+            cases, entries = piece
+            nc.vector.tensor_tensor(dst[:, cases], y[b][:].indirect(offsets[:, entries]), other[:, cases], op)
 
         def look_up_second(b, count):
-            look_up(second[b], b, pos2_sb, log_ratio, ALU.add, count)
+            for piece in pieces(count):
+                look_up(second[b], b, pos2_sb, log_ratio, ALU.add, piece)
 
         def look_up_gap(b, count):
-            look_up(gap[b], b, pos1_sb, second[b], ALU.subtract, count)
-            nc.scalar.activation(gap_abs[b][:], gap[b][:], ACT.Abs)
-            nc.scalar.activation(e_gap[b][:], gap_abs[b][:], ACT.Exp, scale=-1.0)
+            for piece in pieces(count):
+                look_up(gap[b], b, pos1_sb, second[b], ALU.subtract, piece)
 
         def take_larger(b, count):
             for cases, entries in pieces(count):
@@ -209,35 +198,43 @@ def tile_picked_ycox_nll_p_kernel(
 
         def look_up_lag(b, count):
             for cases, entries in pieces(count):
-                nc.vector.tensor_tensor(
-                    lag[b][:, cases], y[b][:].indirect(case_sb[:, entries]), larger[b][:, cases], ALU.subtract
-                )
-                nc.scalar.activation(e_lead[b][:, cases], lag[b][:, cases], ACT.Exp, scale=-1.0)
+                look_up(lag[b], b, case_sb, larger[b], ALU.subtract, (cases, entries))
+                nc.scalar.activation(exp_minus_lag[b][:, cases], lag[b][:, cases], ACT.Exp, scale=-1.0)
 
         look_up_second(first, 2)
         look_up_gap(first, 2)
+        exp_gap0 = case_tile("exp_gap0")
+        exp_minus_gap0 = case_tile("exp_minus_gap0")
+        nc.scalar.activation(exp_gap0[:], gap[first][:], ACT.Exp)
+        nc.scalar.activation(exp_minus_gap0[:], gap[first][:], ACT.Exp, scale=-1.0)
         look_up_second(last, 1)
         take_larger(first, 1)
         look_up_gap(last, 1)
+        abs_gap1 = case_tile("abs_gap1")
+        exp_minus_abs_gap1 = case_tile("exp_minus_abs_gap1")
+        nc.scalar.activation(abs_gap1[:], gap[last][:], ACT.Abs)
+        nc.scalar.activation(exp_minus_abs_gap1[:], abs_gap1[:], ACT.Exp, scale=-1.0)
         look_up_lag(first, 1)
         take_larger(last, 2)
         look_up_lag(last, 2)
 
         pair = [y[last][:, b * V : (b + 1) * V] for b in blocks]
-        controls = [case_tile("controls", b) for b in blocks]
-        for b in blocks:
-            nc.vector.scalar_tensor_tensor(pair[b], e_gap[b][:], 1.0, wgt0[:], ALU.add, ALU.mult)
-        for b in blocks:
+        nc.vector.tensor_tensor(pair[first], exp_gap0[:], exp_minus_gap0[:], ALU.min)
+        nc.vector.scalar_tensor_tensor(pair[last], exp_minus_abs_gap1[:], 1.0, wgt0[:], ALU.add, ALU.mult)
+        nc.vector.scalar_tensor_tensor(pair[first], pair[first], 1.0, wgt0[:], ALU.add, ALU.mult)
+        controls = [case_tile("controls%d" % b) for b in blocks]
+        for b in reversed(blocks):
             nc.vector.scalar_tensor_tensor(
-                controls[b][:], e_lead[b][:], math.exp(LEAD_CAP), pair[b], ALU.min, ALU.mult
+                controls[b][:], exp_minus_lag[b][:], math.exp(EXPONENT_CAP), pair[b], ALU.min, ALU.mult
             )
+        excess = [larger[last - b] for b in blocks]
         for b in blocks:
-            nc.vector.tensor_scalar(pair[b], lag[b][:], LEAD_CAP, 0.0, ALU.add, ALU.min)
+            nc.vector.tensor_scalar(excess[b][:], lag[b][:], EXPONENT_CAP, 0.0, ALU.add, ALU.min)
 
-        for b in blocks:
-            log_sum = case_tile("log_sum", b)
-            result = lag[last - b][:]
+        for b in reversed(blocks):
+            log_sum = case_tile("log_sum%d" % b)
+            result = pair[last - b]
             for cases, entries in pieces(2):
                 nc.scalar.activation(log_sum[:, cases], controls[b][:, cases], ACT.Ln, bias=1.0)
-                nc.vector.tensor_tensor(result[:, cases], log_sum[:, cases], pair[b][:, cases], ALU.subtract)
+                nc.vector.tensor_tensor(result[:, cases], log_sum[:, cases], excess[b][:, cases], ALU.subtract)
             nc.sync.dma_start(out=out[b * P : (b + 1) * P, :], in_=result)

@@ -2,7 +2,6 @@ import math
 from contextlib import ExitStack
 
 import concourse.mybir as mybir
-from concourse.masks import make_identity
 
 K, T, S, V, N, D = 512, 2048, 512, 256, 256, 2
 P = 128
@@ -10,11 +9,10 @@ PACK = 4
 QUADRANT = 32
 LIST_ROWS = 16
 HALF = S // 2
-CASE_TILES = V // P
 LINE_COLUMNS = 4
 BANK_BYTES = 2048
-PRODUCT_BANKS = 5
-EXPONENT_CAP = 30.0
+CAP_BITS = 44
+CAP = CAP_BITS * math.log(2.0)
 FLOPS = 2 * K * N * S
 
 F32 = mybir.dt.float32
@@ -30,14 +28,6 @@ ACT = mybir.ActivationFunctionType
 SCALE_TABLE_AT = 0
 CODE_HALF_BYTES = 4 * HALF
 W_BF0_AT = T
-
-
-def pieces(count):
-    width = V // count
-    return [
-        (slice(i * width, (i + 1) * width), slice(i * width // LIST_ROWS, (i + 1) * width // LIST_ROWS))
-        for i in range(count)
-    ]
 
 
 def tile_picked_ycox_nll_p_kernel(
@@ -69,12 +59,6 @@ def tile_picked_ycox_nll_p_kernel(
                 out=scale_table[QUADRANT * q : QUADRANT * q + PACK, :].bitcast(I32),
                 in_=x_scales[0, PACK * q : PACK * (q + 1), :].bitcast(I32),
             )
-        wgt_rows = keep.tile([P, V], F32, name="wgt_rows")
-        nc.vector.memset(wgt_rows[:], 0.0)
-        nc.sync.dma_start(out=wgt_rows[:D, :], in_=wgt[:, 0, :])
-        identity = keep.tile([P, P], F32, name="identity")
-        nc.vector.memset(identity[:], 0.0)
-        make_identity(nc, identity[:], nomemset=True)
         word_table = keep.tile([P, T], U32, name="word_table", align_bytes=64)
         nc.sync.dma_start(
             out=word_table[:].bitcast(I32),
@@ -83,12 +67,12 @@ def tile_picked_ycox_nll_p_kernel(
         load_w(last)
         pos2_sb = keep.tile([P, V // LIST_ROWS], U16, name="pos2_sb")
         nc.sync.dma_start(pos2_sb[:], pos2)
-        pos1_sb = keep.tile([P, V // LIST_ROWS], U16, name="pos1_sb")
-        nc.sync.dma_start(pos1_sb[:], pos1)
         case_sb = keep.tile([P, V // LIST_ROWS], U16, name="case_sb")
         nc.sync.dma_start(case_sb[:], case)
-        wgt0 = keep.tile([P, V], F32, name="wgt0")
-        nc.sync.dma_start(out=wgt0[:], in_=wgt[0])
+        pos1_sb = keep.tile([P, V // LIST_ROWS], U16, name="pos1_sb")
+        nc.sync.dma_start(pos1_sb[:], pos1)
+        weights = keep.tile([P, D, V], F32, name="weights")
+        nc.sync.dma_start(out=weights[:], in_=wgt.rearrange("d p v -> p d v"))
 
         w_code = [keep.tile([P, P], U32, name="w_code%d" % b, align_bytes=64) for b in blocks]
         w_scale = [keep.tile([P, P], U8, name="w_scale%d" % b, align_bytes=64) for b in blocks]
@@ -112,24 +96,6 @@ def tile_picked_ycox_nll_p_kernel(
         x_scale = shared.tile([P, S], U8, name="x_scale", align_bytes=64, offset=W_BF0_AT)
         nc.vector.tensor_copy(x_scale[:], scale_table[:].indirect(offs_sb[:]))
 
-        wgt_cols = psum.tile([P, CASE_TILES, P], F32, name="wgt_cols", offset=PRODUCT_BANKS * BANK_BYTES)
-        for c in range(CASE_TILES):
-            nc.tensor.transpose(wgt_cols[:, c, :], wgt_rows[:, c * P : (c + 1) * P], identity[:])
-        log_cols = keep.tile([P, CASE_TILES, D], F32, name="log_cols")
-        nc.scalar.activation(log_cols[:], wgt_cols[:, :, :D], ACT.Ln)
-        ratio_cols = keep.tile([P, CASE_TILES], F32, name="ratio_cols", tag="w_bf1", align_bytes=64)
-        for c in range(CASE_TILES):
-            nc.scalar.activation(
-                ratio_cols[:, c : c + 1], log_cols[:, c, 0:1], ACT.Identity, scale=-1.0, bias=log_cols[:, c, 1:2]
-            )
-        ratio_banks = psum.tile([P, PRODUCT_BANKS * BANK_BYTES // 4], F32, name="ratio_banks", offset=0)
-        for c in range(CASE_TILES):
-            nc.tensor.transpose(
-                ratio_banks[:, c * P : (c + 1) * P], ratio_cols[:, c : c + 1].to_broadcast([P, P]), identity[:]
-            )
-        log_ratio = keep.tile([P, V], F32, name="log_ratio")
-        nc.scalar.activation(log_ratio[:], ratio_banks[:, :V], ACT.Copy)
-
         x_code = []
         for h in range(S // HALF):
             code_h = shared.tile(
@@ -141,100 +107,91 @@ def tile_picked_ycox_nll_p_kernel(
 
         w_bf1 = keep.tile([P, P, PACK], BF16, name="w_bf1", align_bytes=64)
         nc.scalar.activation(*cast_views(w_bf1, last), ACT.Copy)
-        quantise_w(w_bf1, last)
 
         y = [keep.tile([P, S], F32, name="y%d" % b) for b in blocks]
 
-        def product(bank, b, h, start, width):
-            cols = slice(h * HALF + start, h * HALF + start + width)
-            acc = psum.tile([P, width], F32, name="acc%d" % bank, offset=bank * BANK_BYTES)
+        def product(b, h):
+            bank = 2 * b + h
+            cols = slice(h * HALF, (h + 1) * HALF)
+            acc = psum.tile([P, HALF], F32, name="acc%d" % bank, offset=bank * BANK_BYTES)
             nc.tensor.matmul_mx(
                 out=acc[:],
                 lhsT=w_code[b][:].bitcast(FP8X4),
                 lhsT_scale=w_scale[b][:],
-                rhs=x_code[h][:, start : start + width].bitcast(FP8X4),
+                rhs=x_code[h][:].bitcast(FP8X4),
                 rhs_scale=x_scale[:, cols],
                 start=True,
                 stop=True,
             )
-            nc.scalar.activation(y[b][:, cols], acc[:], ACT.Copy)
+            return y[b][:, cols], acc[:]
 
-        passes = [
-            (first, 0, 0, HALF),
-            (first, 1, 0, HALF // 2),
-            (first, 1, HALF // 2, HALF // 2),
-            (last, 0, 0, HALF),
-            (last, 1, 0, HALF),
-        ]
-        for bank, one_pass in enumerate(passes):
-            product(bank, *one_pass)
+        nc.vector.tensor_copy(*product(first, 0))
+        nc.scalar.activation(*product(first, 1), ACT.Copy)
+        quantise_w(w_bf1, last)
+        banks1 = [product(last, h) for h in range(2)]
 
         def case_tile(label):
             return keep.tile([P, V], F32, name=label)
 
-        second = [case_tile("second%d" % b) for b in blocks]
+        y2 = [case_tile("y2_%d" % b) for b in blocks]
+        yc = [case_tile("yc_%d" % b) for b in blocks]
         gap = [case_tile("gap%d" % b) for b in blocks]
-        larger = [case_tile("larger%d" % b) for b in blocks]
-        lag = [case_tile("lag%d" % b) for b in blocks]
-        exp_minus_lag = [case_tile("exp_minus_lag%d" % b) for b in blocks]
+        terms_rise = keep.tile([P, D * V + V // 2], F32, name="terms_rise")
+        rise = [case_tile("rise0"), terms_rise[:, D * V - V // 2 :]]
+        lead = [y[last][:, :V], case_tile("lead1")]
+        exp_gap = [
+            keep.tile([P, D, V], F32, name="exp_gap0", tag="yc_0"),
+            keep.tile([P, D, V], F32, name="exp_gap1"),
+        ]
+        exp_lead = [case_tile("exp_lead%d" % b) for b in blocks]
+        halves = [slice(0, V // 2), slice(V // 2, V)]
 
-        def look_up(dst, b, offsets, other, op, piece):
-            cases, entries = piece
-            nc.vector.tensor_tensor(dst[:, cases], y[b][:].indirect(offsets[:, entries]), other[:, cases], op)
+        def exps_of_gap(b):
+            nc.scalar.activation(exp_gap[b][:, 0, :], gap[b][:], ACT.Exp)
+            nc.scalar.activation(exp_gap[b][:, 1, :], gap[b][:], ACT.Exp, scale=-1.0)
 
-        def look_up_second(b, count):
-            for piece in pieces(count):
-                look_up(second[b], b, pos2_sb, log_ratio, ALU.add, piece)
-
-        def look_up_gap(b, count):
-            for piece in pieces(count):
-                look_up(gap[b], b, pos1_sb, second[b], ALU.subtract, piece)
-
-        def take_larger(b, count):
-            for cases, entries in pieces(count):
-                nc.vector.scalar_tensor_tensor(
-                    larger[b][:, cases], gap[b][:, cases], 0.0, second[b][:, cases], ALU.max, ALU.add
-                )
-
-        def look_up_lag(b, count):
-            for cases, entries in pieces(count):
-                look_up(lag[b], b, case_sb, larger[b], ALU.subtract, (cases, entries))
-                nc.scalar.activation(exp_minus_lag[b][:, cases], lag[b][:, cases], ACT.Exp, scale=-1.0)
-
-        look_up_second(first, 2)
-        look_up_gap(first, 2)
-        exp_gap0 = case_tile("exp_gap0")
-        exp_minus_gap0 = case_tile("exp_minus_gap0")
-        nc.scalar.activation(exp_gap0[:], gap[first][:], ACT.Exp)
-        nc.scalar.activation(exp_minus_gap0[:], gap[first][:], ACT.Exp, scale=-1.0)
-        look_up_second(last, 1)
-        take_larger(first, 1)
-        look_up_gap(last, 1)
-        abs_gap1 = case_tile("abs_gap1")
-        exp_minus_abs_gap1 = case_tile("exp_minus_abs_gap1")
-        nc.scalar.activation(abs_gap1[:], gap[last][:], ACT.Abs)
-        nc.scalar.activation(exp_minus_abs_gap1[:], abs_gap1[:], ACT.Exp, scale=-1.0)
-        look_up_lag(first, 1)
-        take_larger(last, 2)
-        look_up_lag(last, 2)
-
-        pair = [y[last][:, b * V : (b + 1) * V] for b in blocks]
-        nc.vector.tensor_tensor(pair[first], exp_gap0[:], exp_minus_gap0[:], ALU.min)
-        nc.vector.scalar_tensor_tensor(pair[last], exp_minus_abs_gap1[:], 1.0, wgt0[:], ALU.add, ALU.mult)
-        nc.vector.scalar_tensor_tensor(pair[first], pair[first], 1.0, wgt0[:], ALU.add, ALU.mult)
-        controls = [case_tile("controls%d" % b) for b in blocks]
-        for b in reversed(blocks):
+        nc.scalar.activation(y2[first][:], y[first][:].indirect(pos2_sb[:]), ACT.Copy)
+        nc.vector.tensor_copy(yc[first][:], y[first][:].indirect(case_sb[:]))
+        nc.vector.tensor_copy(*banks1[0])
+        nc.scalar.activation(*banks1[1], ACT.Copy)
+        nc.vector.tensor_tensor(gap[first][:], y[first][:].indirect(pos1_sb[:]), y2[first][:], ALU.subtract)
+        nc.scalar.activation(y2[last][:], y[last][:].indirect(pos2_sb[:]), ACT.Copy)
+        nc.vector.tensor_tensor(rise[first][:], yc[first][:], y2[first][:], ALU.subtract)
+        nc.scalar.activation(yc[last][:], y[last][:].indirect(case_sb[:]), ACT.Copy)
+        nc.vector.tensor_tensor(gap[last][:], y[last][:].indirect(pos1_sb[:]), y2[last][:], ALU.subtract)
+        exps_of_gap(first)
+        nc.vector.tensor_tensor(rise[last][:], yc[last][:], y2[last][:], ALU.subtract)
+        nc.vector.scalar_tensor_tensor(lead[first][:], gap[first][:], 0.0, rise[first][:], ALU.max, ALU.subtract)
+        exps_of_gap(last)
+        nc.scalar.activation(exp_lead[first][:], lead[first][:], ACT.Exp)
+        for cases in halves:
             nc.vector.scalar_tensor_tensor(
-                controls[b][:], exp_minus_lag[b][:], math.exp(EXPONENT_CAP), pair[b], ALU.min, ALU.mult
+                lead[last][:, cases], gap[last][:, cases], 0.0, rise[last][:, cases], ALU.max, ALU.subtract
             )
-        excess = [larger[last - b] for b in blocks]
-        for b in blocks:
-            nc.vector.tensor_scalar(excess[b][:], lag[b][:], EXPONENT_CAP, 0.0, ALU.add, ALU.min)
+            nc.scalar.activation(exp_lead[last][:, cases], lead[last][:, cases], ACT.Exp)
 
-        for b in reversed(blocks):
+        terms = [
+            terms_rise[:, : D * V].rearrange("p (d v) -> p d v", d=D),
+            keep.tile([P, D, V], F32, name="terms1"),
+        ]
+        pair = [case_tile("pair%d" % b) for b in blocks]
+        controls = [case_tile("controls%d" % b) for b in blocks]
+        for b in blocks:
+            nc.vector.scalar_tensor_tensor(terms[b][:], exp_gap[b][:], 1.0, weights[:], ALU.min, ALU.mult)
+        for b in blocks:
+            nc.vector.tensor_tensor(pair[b][:], terms[b][:, 0, :], terms[b][:, 1, :], ALU.add)
+        for b in blocks:
+            nc.vector.scalar_tensor_tensor(
+                controls[b][:], exp_lead[b][:], 2.0**CAP_BITS, pair[b][:], ALU.min, ALU.mult
+            )
+        for b in blocks:
             log_sum = case_tile("log_sum%d" % b)
-            result = pair[last - b]
-            for cases, entries in pieces(2):
-                nc.scalar.activation(log_sum[:, cases], controls[b][:, cases], ACT.Ln, bias=1.0)
-                nc.vector.tensor_tensor(result[:, cases], log_sum[:, cases], excess[b][:, cases], ALU.subtract)
-            nc.sync.dma_start(out=out[b * P : (b + 1) * P, :], in_=result)
+            result = case_tile("result%d" % b)
+            for cases in halves:
+                nc.scalar.activation(
+                    log_sum[:, cases], controls[b][:, cases], ACT.Ln, bias=2.0**-CAP_BITS, scale=2.0**-CAP_BITS
+                )
+                nc.vector.scalar_tensor_tensor(
+                    result[:, cases], lead[b][:, cases], CAP, log_sum[:, cases], ALU.max, ALU.add
+                )
+            nc.sync.dma_start(out=out[b * P : (b + 1) * P, :], in_=result[:])

@@ -26,7 +26,6 @@ ALU = mybir.AluOpType
 ACT = mybir.ActivationFunctionType
 
 SCALE_TABLE_AT = 0
-CODE_HALF_BYTES = 4 * HALF
 W_BF0_AT = T
 
 
@@ -74,7 +73,10 @@ def tile_picked_ycox_nll_p_kernel(
         weights = keep.tile([P, D, V], F32, name="weights")
         nc.sync.dma_start(out=weights[:], in_=wgt.rearrange("d p v -> p d v"))
 
-        w_code = [keep.tile([P, P], U32, name="w_code%d" % b, align_bytes=64) for b in blocks]
+        w_code = [
+            keep.tile([P, P], U32, name="w_code0", align_bytes=64),
+            keep.tile([P, P], U32, name="w_code1", align_bytes=64, tag="chain"),
+        ]
         w_scale = [keep.tile([P, P], U8, name="w_scale%d" % b, align_bytes=64) for b in blocks]
 
         def cast_views(w_bf, b):
@@ -96,51 +98,48 @@ def tile_picked_ycox_nll_p_kernel(
         x_scale = shared.tile([P, S], U8, name="x_scale", align_bytes=64, offset=W_BF0_AT)
         nc.vector.tensor_copy(x_scale[:], scale_table[:].indirect(offs_sb[:]))
 
-        x_code = []
-        for h in range(S // HALF):
-            code_h = shared.tile(
-                [P, HALF], U32, name="x_code%d" % h, align_bytes=64, offset=SCALE_TABLE_AT + h * CODE_HALF_BYTES
-            )
-            entries = slice(h * HALF // LIST_ROWS, (h + 1) * HALF // LIST_ROWS)
-            nc.vector.tensor_copy(code_h[:], word_table[:].indirect(offs_sb[:, entries]))
-            x_code.append(code_h)
+        x_code = shared.tile([P, S], U32, name="x_code", align_bytes=64, offset=SCALE_TABLE_AT)
+        half0, half1 = slice(0, HALF), slice(HALF, S)
+        quarter2, quarter3 = slice(HALF, HALF + S // 4), slice(HALF + S // 4, S)
+        for cols in (half0, quarter2, quarter3):
+            entries = slice(cols.start // LIST_ROWS, cols.stop // LIST_ROWS)
+            nc.vector.tensor_copy(x_code[:, cols], word_table[:].indirect(offs_sb[:, entries]))
 
         w_bf1 = keep.tile([P, P, PACK], BF16, name="w_bf1", align_bytes=64)
         nc.scalar.activation(*cast_views(w_bf1, last), ACT.Copy)
 
         y = [keep.tile([P, S], F32, name="y%d" % b) for b in blocks]
 
-        def product(b, h):
-            bank = 2 * b + h
-            cols = slice(h * HALF, (h + 1) * HALF)
-            acc = psum.tile([P, HALF], F32, name="acc%d" % bank, offset=bank * BANK_BYTES)
+        def product(bank, b, cols):
+            acc = psum.tile([P, cols.stop - cols.start], F32, name="acc%d" % bank, offset=bank * BANK_BYTES)
             nc.tensor.matmul_mx(
                 out=acc[:],
                 lhsT=w_code[b][:].bitcast(FP8X4),
                 lhsT_scale=w_scale[b][:],
-                rhs=x_code[h][:].bitcast(FP8X4),
+                rhs=x_code[:, cols].bitcast(FP8X4),
                 rhs_scale=x_scale[:, cols],
                 start=True,
                 stop=True,
             )
             return y[b][:, cols], acc[:]
 
-        nc.vector.tensor_copy(*product(first, 0))
-        nc.scalar.activation(*product(first, 1), ACT.Copy)
+        nc.scalar.activation(*product(0, first, half0), ACT.Copy)
+        nc.scalar.activation(*product(1, first, quarter2), ACT.Copy)
+        nc.scalar.activation(*product(2, first, quarter3), ACT.Copy)
         quantise_w(w_bf1, last)
-        banks1 = [product(last, h) for h in range(2)]
+        banks1 = [product(3, last, half0), product(4, last, half1)]
 
         def case_tile(label):
             return keep.tile([P, V], F32, name=label)
 
         y2 = [case_tile("y2_%d" % b) for b in blocks]
-        yc = [case_tile("yc_%d" % b) for b in blocks]
+        yc = [keep.tile([P, V], F32, name="yc_0", align_bytes=64, tag="chain"), case_tile("yc_1")]
         gap = [case_tile("gap%d" % b) for b in blocks]
         terms_rise = keep.tile([P, D * V + V // 2], F32, name="terms_rise")
         rise = [case_tile("rise0"), terms_rise[:, D * V - V // 2 :]]
         lead = [y[last][:, :V], case_tile("lead1")]
         exp_gap = [
-            keep.tile([P, D, V], F32, name="exp_gap0", tag="yc_0"),
+            keep.tile([P, D, V], F32, name="exp_gap0", align_bytes=64, tag="chain"),
             keep.tile([P, D, V], F32, name="exp_gap1"),
         ]
         exp_lead = [case_tile("exp_lead%d" % b) for b in blocks]
@@ -151,9 +150,9 @@ def tile_picked_ycox_nll_p_kernel(
             nc.scalar.activation(exp_gap[b][:, 1, :], gap[b][:], ACT.Exp, scale=-1.0)
 
         nc.scalar.activation(y2[first][:], y[first][:].indirect(pos2_sb[:]), ACT.Copy)
-        nc.vector.tensor_copy(yc[first][:], y[first][:].indirect(case_sb[:]))
         nc.vector.tensor_copy(*banks1[0])
-        nc.scalar.activation(*banks1[1], ACT.Copy)
+        nc.vector.tensor_copy(*banks1[1])
+        nc.vector.tensor_copy(yc[first][:], y[first][:].indirect(case_sb[:]))
         nc.vector.tensor_tensor(gap[first][:], y[first][:].indirect(pos1_sb[:]), y2[first][:], ALU.subtract)
         nc.scalar.activation(y2[last][:], y[last][:].indirect(pos2_sb[:]), ACT.Copy)
         nc.vector.tensor_tensor(rise[first][:], yc[first][:], y2[first][:], ALU.subtract)

@@ -26,7 +26,6 @@ ALU = mybir.AluOpType
 ACT = mybir.ActivationFunctionType
 
 SCALE_TABLE_AT = 0
-W_BF0_AT = T
 
 
 def tile_picked_ycox_nll_p_kernel(
@@ -42,6 +41,8 @@ def tile_picked_ycox_nll_p_kernel(
 
         scale_table = shared.tile([P, T], U8, name="scale_table", align_bytes=64, offset=SCALE_TABLE_AT)
         nc.vector.memset(scale_table[:].bitcast(I32), 0)
+        x_scale = keep.tile([P, S], U8, name="x_scale", align_bytes=64)
+        nc.vector.memset(x_scale[:].bitcast(I32), 0)
         w_raw = [keep.tile([P, PACK, P], F32, name="w_raw%d" % b) for b in blocks]
 
         def load_w(b):
@@ -52,26 +53,21 @@ def tile_picked_ycox_nll_p_kernel(
         load_w(first)
         offs_sb = keep.tile([P, S // LIST_ROWS], U16, name="offs_sb")
         nc.sync.dma_start(offs_sb[:], offs)
-        for q in range(P // QUADRANT):
-            queue = nc.sync if q % 2 == 0 else nc.scalar
-            queue.dma_start(
-                out=scale_table[QUADRANT * q : QUADRANT * q + PACK, :].bitcast(I32),
-                in_=x_scales[0, PACK * q : PACK * (q + 1), :].bitcast(I32),
-            )
+        pos2_sb = keep.tile([P, V // LIST_ROWS], U16, name="pos2_sb")
+        nc.sync.dma_start(pos2_sb[:], pos2)
+        case_sb = keep.tile([P, V // LIST_ROWS], U16, name="case_sb")
+        nc.sync.dma_start(case_sb[:], case)
+        nc.sync.dma_start(
+            out=scale_table[QUADRANT : 3 * QUADRANT : PACK, :].bitcast(I32), in_=x_scales[0].bitcast(I32)
+        )
         word_table = keep.tile([P, T], U32, name="word_table", align_bytes=64)
         nc.sync.dma_start(
             out=word_table[:].bitcast(I32),
             in_=x_words[0].rearrange("p c t -> p (c t)").bitcast(I32),
         )
         load_w(last)
-        pos2_sb = keep.tile([P, V // LIST_ROWS], U16, name="pos2_sb")
-        nc.sync.dma_start(pos2_sb[:], pos2)
-        case_sb = keep.tile([P, V // LIST_ROWS], U16, name="case_sb")
-        nc.sync.dma_start(case_sb[:], case)
         pos1_sb = keep.tile([P, V // LIST_ROWS], U16, name="pos1_sb")
         nc.sync.dma_start(pos1_sb[:], pos1)
-        weights = keep.tile([P, D, V], F32, name="weights")
-        nc.sync.dma_start(out=weights[:], in_=wgt.rearrange("d p v -> p d v"))
 
         w_code = [
             keep.tile([P, P], U32, name="w_code0", align_bytes=64),
@@ -92,20 +88,23 @@ def tile_picked_ycox_nll_p_kernel(
                 in_=w_bf[:].rearrange("p m t -> p (m t)"),
             )
 
-        w_bf0 = shared.tile([P, P, PACK], BF16, name="w_bf0", align_bytes=64, offset=W_BF0_AT)
-        nc.vector.tensor_copy(*cast_views(w_bf0, first))
+        picked_scale = keep.tile([P, S], U8, name="picked_scale", align_bytes=64, tag="weights")
+        nc.vector.tensor_copy(picked_scale[:], scale_table[:].indirect(offs_sb[:]))
+        for j in range(PACK):
+            rows = slice(QUADRANT + PACK * j, 3 * QUADRANT, PACK * PACK)
+            nc.scalar.dma_start(out=x_scale[j:P:QUADRANT, :].bitcast(I32), in_=picked_scale[rows, :].bitcast(I32))
+        w_bf0 = keep.tile([P, P, PACK], BF16, name="w_bf0", align_bytes=64)
+        nc.scalar.activation(*cast_views(w_bf0, first), ACT.Copy)
         quantise_w(w_bf0, first)
-        x_scale = shared.tile([P, S], U8, name="x_scale", align_bytes=64, offset=W_BF0_AT)
-        nc.vector.tensor_copy(x_scale[:], scale_table[:].indirect(offs_sb[:]))
 
-        x_code = shared.tile([P, S], U32, name="x_code", align_bytes=64, offset=SCALE_TABLE_AT)
+        x_code = shared.tile([P, S], U32, name="x_code", align_bytes=64, offset=SCALE_TABLE_AT + T // 2)
         half0, half1 = slice(0, HALF), slice(HALF, S)
         quarter2, quarter3 = slice(HALF, HALF + S // 4), slice(HALF + S // 4, S)
         for cols in (half0, quarter2, quarter3):
             entries = slice(cols.start // LIST_ROWS, cols.stop // LIST_ROWS)
             nc.vector.tensor_copy(x_code[:, cols], word_table[:].indirect(offs_sb[:, entries]))
 
-        w_bf1 = keep.tile([P, P, PACK], BF16, name="w_bf1", align_bytes=64)
+        w_bf1 = shared.tile([P, P, PACK], BF16, name="w_bf1", align_bytes=64, offset=SCALE_TABLE_AT)
         nc.scalar.activation(*cast_views(w_bf1, last), ACT.Copy)
 
         y = [keep.tile([P, S], F32, name="y%d" % b) for b in blocks]
@@ -127,6 +126,8 @@ def tile_picked_ycox_nll_p_kernel(
         nc.scalar.activation(*product(1, first, quarter2), ACT.Copy)
         nc.scalar.activation(*product(2, first, quarter3), ACT.Copy)
         quantise_w(w_bf1, last)
+        weights = keep.tile([P, D, V], F32, name="weights", align_bytes=64)
+        nc.sync.dma_start(out=weights[:], in_=wgt.rearrange("d p v -> p d v"))
         banks1 = [product(3, last, half0), product(4, last, half1)]
 
         def case_tile(label):
@@ -193,4 +194,5 @@ def tile_picked_ycox_nll_p_kernel(
                 nc.vector.scalar_tensor_tensor(
                     result[:, cases], lead[b][:, cases], CAP, log_sum[:, cases], ALU.max, ALU.add
                 )
-            nc.sync.dma_start(out=out[b * P : (b + 1) * P, :], in_=result[:])
+                queue = nc.scalar if (b, cases) == (last, halves[1]) else nc.sync
+                queue.dma_start(out=out[b * P : (b + 1) * P, cases], in_=result[:, cases])

@@ -194,5 +194,4 @@ def tile_picked_ycox_nll_p_kernel(
                 nc.vector.scalar_tensor_tensor(
                     result[:, cases], lead[b][:, cases], CAP, log_sum[:, cases], ALU.max, ALU.add
                 )
-                queue = nc.scalar if (b, cases) == (last, halves[1]) else nc.sync
-                queue.dma_start(out=out[b * P : (b + 1) * P, cases], in_=result[:, cases])
+            nc.sync.dma_start(out=out[b * P : (b + 1) * P, :], in_=result[:])

@@ -8,7 +8,7 @@ P = 128
 PACK = 4
 QUADRANT = 32
 LIST_ROWS = 16
-HALF = S // 2
+QUARTER = S // 4
 LINE_COLUMNS = 4
 BANK_BYTES = 2048
 CAP_BITS = 44
@@ -43,42 +43,37 @@ def tile_picked_ycox_nll_p_kernel(
         nc.vector.memset(scale_table[:].bitcast(I32), 0)
         x_scale = keep.tile([P, S], U8, name="x_scale", align_bytes=64)
         nc.vector.memset(x_scale[:].bitcast(I32), 0)
-        w_raw = [keep.tile([P, PACK, P], F32, name="w_raw%d" % b) for b in blocks]
-
-        def load_w(b):
-            nc.sync.dma_start(
-                out=w_raw[b][:], in_=w1[:, b * P : (b + 1) * P].rearrange("(p t) m -> p t m", t=PACK)
-            )
-
-        load_w(first)
+        w_raw = keep.tile([P, PACK, N], F32, name="w_raw")
+        w_rows = w1.rearrange("(p t) m -> p t m", t=PACK)
+        nc.sync.dma_start(out=w_raw[:, :1, :], in_=w_rows[:, :1, :])
         offs_sb = keep.tile([P, S // LIST_ROWS], U16, name="offs_sb")
         nc.sync.dma_start(offs_sb[:], offs)
-        pos2_sb = keep.tile([P, V // LIST_ROWS], U16, name="pos2_sb")
-        nc.sync.dma_start(pos2_sb[:], pos2)
-        case_sb = keep.tile([P, V // LIST_ROWS], U16, name="case_sb")
-        nc.sync.dma_start(case_sb[:], case)
         nc.sync.dma_start(
             out=scale_table[QUADRANT : 3 * QUADRANT : PACK, :].bitcast(I32), in_=x_scales[0].bitcast(I32)
         )
+        nc.sync.dma_start(out=w_raw[:, 1:, :], in_=w_rows[:, 1:, :])
         word_table = keep.tile([P, T], U32, name="word_table", align_bytes=64)
         nc.sync.dma_start(
             out=word_table[:].bitcast(I32),
             in_=x_words[0].rearrange("p c t -> p (c t)").bitcast(I32),
         )
-        load_w(last)
+        pos2_sb = keep.tile([P, V // LIST_ROWS], U16, name="pos2_sb")
+        nc.sync.dma_start(pos2_sb[:], pos2)
+        case_sb = keep.tile([P, V // LIST_ROWS], U16, name="case_sb")
+        nc.sync.dma_start(case_sb[:], case)
         pos1_sb = keep.tile([P, V // LIST_ROWS], U16, name="pos1_sb")
         nc.sync.dma_start(pos1_sb[:], pos1)
 
         w_code = [
             keep.tile([P, P], U32, name="w_code0", align_bytes=64),
-            keep.tile([P, P], U32, name="w_code1", align_bytes=64, tag="chain"),
+            keep.tile([P, P], U32, name="w_code1", align_bytes=64),
         ]
         w_scale = [keep.tile([P, P], U8, name="w_scale%d" % b, align_bytes=64) for b in blocks]
 
         def cast_views(w_bf, b):
             return (
                 w_bf[:].rearrange("p (c i) t -> p c t i", i=LINE_COLUMNS),
-                w_raw[b][:].rearrange("p t (c i) -> p c t i", i=LINE_COLUMNS),
+                w_raw[:, :, b * P : (b + 1) * P].rearrange("p t (c i) -> p c t i", i=LINE_COLUMNS),
             )
 
         def quantise_w(w_bf, b):
@@ -94,18 +89,17 @@ def tile_picked_ycox_nll_p_kernel(
             rows = slice(QUADRANT + PACK * j, 3 * QUADRANT, PACK * PACK)
             nc.scalar.dma_start(out=x_scale[j:P:QUADRANT, :].bitcast(I32), in_=picked_scale[rows, :].bitcast(I32))
         w_bf0 = keep.tile([P, P, PACK], BF16, name="w_bf0", align_bytes=64)
-        nc.scalar.activation(*cast_views(w_bf0, first), ACT.Copy)
+        nc.vector.tensor_copy(*cast_views(w_bf0, first))
+        w_bf1 = shared.tile([P, P, PACK], BF16, name="w_bf1", align_bytes=64, offset=SCALE_TABLE_AT)
+        nc.vector.tensor_copy(*cast_views(w_bf1, last))
         quantise_w(w_bf0, first)
+        quantise_w(w_bf1, last)
 
         x_code = shared.tile([P, S], U32, name="x_code", align_bytes=64, offset=SCALE_TABLE_AT + T // 2)
-        half0, half1 = slice(0, HALF), slice(HALF, S)
-        quarter2, quarter3 = slice(HALF, HALF + S // 4), slice(HALF + S // 4, S)
-        for cols in (half0, quarter2, quarter3):
+        quarters = [slice(q * QUARTER, (q + 1) * QUARTER) for q in range(S // QUARTER)]
+        for cols in quarters:
             entries = slice(cols.start // LIST_ROWS, cols.stop // LIST_ROWS)
             nc.vector.tensor_copy(x_code[:, cols], word_table[:].indirect(offs_sb[:, entries]))
-
-        w_bf1 = shared.tile([P, P, PACK], BF16, name="w_bf1", align_bytes=64, offset=SCALE_TABLE_AT)
-        nc.scalar.activation(*cast_views(w_bf1, last), ACT.Copy)
 
         y = [keep.tile([P, S], F32, name="y%d" % b) for b in blocks]
 
@@ -122,13 +116,15 @@ def tile_picked_ycox_nll_p_kernel(
             )
             return y[b][:, cols], acc[:]
 
-        nc.scalar.activation(*product(0, first, half0), ACT.Copy)
-        nc.scalar.activation(*product(1, first, quarter2), ACT.Copy)
-        nc.scalar.activation(*product(2, first, quarter3), ACT.Copy)
-        quantise_w(w_bf1, last)
+        for q, cols in enumerate(quarters):
+            for b in blocks:
+                made = product(len(blocks) * q + b, b, cols)
+                if b == first and cols == quarters[-1]:
+                    nc.vector.tensor_copy(*made)
+                else:
+                    nc.scalar.activation(*made, ACT.Copy)
         weights = keep.tile([P, D, V], F32, name="weights", align_bytes=64)
         nc.sync.dma_start(out=weights[:], in_=wgt.rearrange("d p v -> p d v"))
-        banks1 = [product(3, last, half0), product(4, last, half1)]
 
         def case_tile(label):
             return keep.tile([P, V], F32, name=label)
@@ -150,11 +146,13 @@ def tile_picked_ycox_nll_p_kernel(
             nc.scalar.activation(exp_gap[b][:, 0, :], gap[b][:], ACT.Exp)
             nc.scalar.activation(exp_gap[b][:, 1, :], gap[b][:], ACT.Exp, scale=-1.0)
 
-        nc.scalar.activation(y2[first][:], y[first][:].indirect(pos2_sb[:]), ACT.Copy)
-        nc.vector.tensor_copy(*banks1[0])
-        nc.vector.tensor_copy(*banks1[1])
         nc.vector.tensor_copy(yc[first][:], y[first][:].indirect(case_sb[:]))
-        nc.vector.tensor_tensor(gap[first][:], y[first][:].indirect(pos1_sb[:]), y2[first][:], ALU.subtract)
+        for cases in halves:
+            entries = slice(cases.start // LIST_ROWS, cases.stop // LIST_ROWS)
+            nc.scalar.activation(y2[first][:, cases], y[first][:].indirect(pos2_sb[:, entries]), ACT.Copy)
+            nc.vector.tensor_tensor(
+                gap[first][:, cases], y[first][:].indirect(pos1_sb[:, entries]), y2[first][:, cases], ALU.subtract
+            )
         nc.scalar.activation(y2[last][:], y[last][:].indirect(pos2_sb[:]), ACT.Copy)
         nc.vector.tensor_tensor(rise[first][:], yc[first][:], y2[first][:], ALU.subtract)
         nc.scalar.activation(yc[last][:], y[last][:].indirect(case_sb[:]), ACT.Copy)

@@ -11,7 +11,7 @@ LIST_ROWS = 16
 QUARTER = S // 4
 LINE_COLUMNS = 4
 BANK_BYTES = 2048
-CAP_BITS = 44
+CAP_BITS = 40
 CAP = CAP_BITS * math.log(2.0)
 FLOPS = 2 * K * N * S
 
@@ -129,67 +129,57 @@ def tile_picked_ycox_nll_p_kernel(
         def case_tile(label):
             return keep.tile([P, V], F32, name=label)
 
+        yc = [case_tile("yc%d" % b) for b in blocks]
         y2 = [case_tile("y2_%d" % b) for b in blocks]
-        yc = [keep.tile([P, V], F32, name="yc_0", align_bytes=64, tag="chain"), case_tile("yc_1")]
-        gap = [case_tile("gap%d" % b) for b in blocks]
-        terms_rise = keep.tile([P, D * V + V // 2], F32, name="terms_rise")
-        rise = [case_tile("rise0"), terms_rise[:, D * V - V // 2 :]]
-        lead = [y[last][:, :V], case_tile("lead1")]
-        exp_gap = [
-            keep.tile([P, D, V], F32, name="exp_gap0", align_bytes=64, tag="chain"),
-            keep.tile([P, D, V], F32, name="exp_gap1"),
+        lift1 = [case_tile("lift1_%d" % b) for b in blocks]
+        lift2 = [case_tile("lift2_%d" % b) for b in blocks]
+        exps = [
+            y[last][:].rearrange("p (d v) -> p d v", d=D),
+            keep.tile([P, D, V], F32, name="exps1"),
         ]
-        exp_lead = [case_tile("exp_lead%d" % b) for b in blocks]
         halves = [slice(0, V // 2), slice(V // 2, V)]
 
-        def exps_of_gap(b):
-            nc.scalar.activation(exp_gap[b][:, 0, :], gap[b][:], ACT.Exp)
-            nc.scalar.activation(exp_gap[b][:, 1, :], gap[b][:], ACT.Exp, scale=-1.0)
+        def drop(b, cases):
+            nc.vector.scalar_tensor_tensor(
+                exps[b][:, 0, cases], lift2[b][:, cases], CAP, lift1[b][:, cases], ALU.max, ALU.subtract
+            )
+            nc.scalar.activation(exps[b][:, 0, cases], exps[b][:, 0, cases], ACT.Exp, scale=-1.0)
 
-        nc.vector.tensor_copy(yc[first][:], y[first][:].indirect(case_sb[:]))
+        nc.vector.tensor_copy(y2[first][:], y[first][:].indirect(pos2_sb[:]))
         for cases in halves:
             entries = slice(cases.start // LIST_ROWS, cases.stop // LIST_ROWS)
-            nc.scalar.activation(y2[first][:, cases], y[first][:].indirect(pos2_sb[:, entries]), ACT.Copy)
+            nc.scalar.activation(yc[first][:, cases], y[first][:].indirect(case_sb[:, entries]), ACT.Copy)
             nc.vector.tensor_tensor(
-                gap[first][:, cases], y[first][:].indirect(pos1_sb[:, entries]), y2[first][:, cases], ALU.subtract
+                lift1[first][:, cases], y[first][:].indirect(pos1_sb[:, entries]), yc[first][:, cases], ALU.subtract
             )
-        nc.scalar.activation(y2[last][:], y[last][:].indirect(pos2_sb[:]), ACT.Copy)
-        nc.vector.tensor_tensor(rise[first][:], yc[first][:], y2[first][:], ALU.subtract)
         nc.scalar.activation(yc[last][:], y[last][:].indirect(case_sb[:]), ACT.Copy)
-        nc.vector.tensor_tensor(gap[last][:], y[last][:].indirect(pos1_sb[:]), y2[last][:], ALU.subtract)
-        exps_of_gap(first)
-        nc.vector.tensor_tensor(rise[last][:], yc[last][:], y2[last][:], ALU.subtract)
-        nc.vector.scalar_tensor_tensor(lead[first][:], gap[first][:], 0.0, rise[first][:], ALU.max, ALU.subtract)
-        exps_of_gap(last)
-        nc.scalar.activation(exp_lead[first][:], lead[first][:], ACT.Exp)
+        nc.vector.tensor_tensor(lift2[first][:], y2[first][:], yc[first][:], ALU.subtract)
+        nc.scalar.activation(y2[last][:], y[last][:].indirect(pos2_sb[:]), ACT.Copy)
+        nc.vector.tensor_tensor(lift1[last][:], y[last][:].indirect(pos1_sb[:]), yc[last][:], ALU.subtract)
+        nc.vector.tensor_tensor(lift2[last][:], y2[last][:], yc[last][:], ALU.subtract)
+        for b in blocks:
+            nc.scalar.activation(exps[b][:, 1, :], lift2[b][:], ACT.Exp)
+        drop(first, slice(0, V))
         for cases in halves:
-            nc.vector.scalar_tensor_tensor(
-                lead[last][:, cases], gap[last][:, cases], 0.0, rise[last][:, cases], ALU.max, ALU.subtract
-            )
-            nc.scalar.activation(exp_lead[last][:, cases], lead[last][:, cases], ACT.Exp)
+            drop(last, cases)
 
-        terms = [
-            terms_rise[:, : D * V].rearrange("p (d v) -> p d v", d=D),
-            keep.tile([P, D, V], F32, name="terms1"),
-        ]
-        pair = [case_tile("pair%d" % b) for b in blocks]
+        terms = [keep.tile([P, D, V], F32, name="terms%d" % b) for b in blocks]
         controls = [case_tile("controls%d" % b) for b in blocks]
         for b in blocks:
-            nc.vector.scalar_tensor_tensor(terms[b][:], exp_gap[b][:], 1.0, weights[:], ALU.min, ALU.mult)
-        for b in blocks:
-            nc.vector.tensor_tensor(pair[b][:], terms[b][:, 0, :], terms[b][:, 1, :], ALU.add)
+            nc.vector.scalar_tensor_tensor(terms[b][:], exps[b][:], 2.0**CAP_BITS, weights[:], ALU.min, ALU.mult)
         for b in blocks:
             nc.vector.scalar_tensor_tensor(
-                controls[b][:], exp_lead[b][:], 2.0**CAP_BITS, pair[b][:], ALU.min, ALU.mult
+                controls[b][:], terms[b][:, 1, :], 2.0**-CAP_BITS, terms[b][:, 0, :], ALU.mult, ALU.add
             )
+        top = [exps[b][:, 0, :] for b in blocks]
+        for b in blocks:
+            nc.vector.scalar_tensor_tensor(top[b], lift1[b][:], -CAP, lift2[b][:], ALU.add, ALU.max)
         for b in blocks:
             log_sum = case_tile("log_sum%d" % b)
             result = case_tile("result%d" % b)
             for cases in halves:
-                nc.scalar.activation(
-                    log_sum[:, cases], controls[b][:, cases], ACT.Ln, bias=2.0**-CAP_BITS, scale=2.0**-CAP_BITS
-                )
+                nc.scalar.activation(log_sum[:, cases], controls[b][:, cases], ACT.Ln, bias=2.0**-CAP_BITS)
                 nc.vector.scalar_tensor_tensor(
-                    result[:, cases], lead[b][:, cases], CAP, log_sum[:, cases], ALU.max, ALU.add
+                    result[:, cases], top[b][:, cases], CAP, log_sum[:, cases], ALU.max, ALU.add
                 )
             nc.sync.dma_start(out=out[b * P : (b + 1) * P, :], in_=result[:])

@@ -45,13 +45,13 @@ def tile_picked_ycox_nll_p_kernel(
         nc.vector.memset(x_scale[:].bitcast(I32), 0)
         w_raw = keep.tile([P, PACK, N], F32, name="w_raw")
         w_rows = w1.rearrange("(p t) m -> p t m", t=PACK)
-        nc.sync.dma_start(out=w_raw[:, :1, :], in_=w_rows[:, :1, :])
+        nc.sync.dma_start(out=w_raw[:, : PACK // 2, :], in_=w_rows[:, : PACK // 2, :])
         offs_sb = keep.tile([P, S // LIST_ROWS], U16, name="offs_sb")
         nc.sync.dma_start(offs_sb[:], offs)
         nc.sync.dma_start(
             out=scale_table[QUADRANT : 3 * QUADRANT : PACK, :].bitcast(I32), in_=x_scales[0].bitcast(I32)
         )
-        nc.sync.dma_start(out=w_raw[:, 1:, :], in_=w_rows[:, 1:, :])
+        nc.sync.dma_start(out=w_raw[:, PACK // 2 :, :], in_=w_rows[:, PACK // 2 :, :])
         word_table = keep.tile([P, T], U32, name="word_table", align_bytes=64)
         nc.sync.dma_start(
             out=word_table[:].bitcast(I32),

@@ -87,7 +87,7 @@ def tile_picked_ycox_nll_p_kernel(
         nc.vector.tensor_copy(picked_scale[:], scale_table[:].indirect(offs_sb[:]))
         for j in range(PACK):
             rows = slice(QUADRANT + PACK * j, 3 * QUADRANT, PACK * PACK)
-            nc.scalar.dma_start(out=x_scale[j:P:QUADRANT, :].bitcast(I32), in_=picked_scale[rows, :].bitcast(I32))
+            nc.sync.dma_start(out=x_scale[j:P:QUADRANT, :].bitcast(I32), in_=picked_scale[rows, :].bitcast(I32))
         w_bf0 = keep.tile([P, P, PACK], BF16, name="w_bf0", align_bytes=64)
         nc.vector.tensor_copy(*cast_views(w_bf0, first))
         w_bf1 = shared.tile([P, P, PACK], BF16, name="w_bf1", align_bytes=64, offset=SCALE_TABLE_AT)

@@ -119,7 +119,7 @@ def tile_picked_ycox_nll_p_kernel(
         for q, cols in enumerate(quarters):
             for b in blocks:
                 made = product(len(blocks) * q + b, b, cols)
-                if b == first and cols == quarters[-1]:
+                if b == last and cols == quarters[-2]:
                     nc.vector.tensor_copy(*made)
                 else:
                     nc.scalar.activation(*made, ACT.Copy)
@@ -134,8 +134,7 @@ def tile_picked_ycox_nll_p_kernel(
         lift1 = [case_tile("lift1_%d" % b) for b in blocks]
         lift2 = [case_tile("lift2_%d" % b) for b in blocks]
         exps = [
-            y[last][:].rearrange("p (d v) -> p d v", d=D),
-            keep.tile([P, D, V], F32, name="exps1"),
+            keep.tile([P, D, V], F32, name="exps%d" % b) for b in blocks
         ]
         halves = [slice(0, V // 2), slice(V // 2, V)]
 
@@ -155,11 +154,20 @@ def tile_picked_ycox_nll_p_kernel(
         nc.scalar.activation(yc[last][:], y[last][:].indirect(case_sb[:]), ACT.Copy)
         nc.vector.tensor_tensor(lift2[first][:], y2[first][:], yc[first][:], ALU.subtract)
         nc.scalar.activation(y2[last][:], y[last][:].indirect(pos2_sb[:]), ACT.Copy)
-        nc.vector.tensor_tensor(lift1[last][:], y[last][:].indirect(pos1_sb[:]), yc[last][:], ALU.subtract)
-        nc.vector.tensor_tensor(lift2[last][:], y2[last][:], yc[last][:], ALU.subtract)
-        for b in blocks:
-            nc.scalar.activation(exps[b][:, 1, :], lift2[b][:], ACT.Exp)
+        early, late = halves
+        y1_late = keep.tile([P, V // 2], F32, name="y1_late")
+        nc.scalar.activation(y1_late[:], y[last][:].indirect(pos1_sb[:, late.start // LIST_ROWS :]), ACT.Copy)
+        nc.vector.tensor_tensor(
+            lift1[last][:, early],
+            y[last][:].indirect(pos1_sb[:, : early.stop // LIST_ROWS]),
+            yc[last][:, early],
+            ALU.subtract,
+        )
+        nc.scalar.activation(exps[first][:, 1, :], lift2[first][:], ACT.Exp)
         drop(first, slice(0, V))
+        nc.vector.tensor_tensor(lift2[last][:], y2[last][:], yc[last][:], ALU.subtract)
+        nc.vector.tensor_tensor(lift1[last][:, late], y1_late[:], yc[last][:, late], ALU.subtract)
+        nc.scalar.activation(exps[last][:, 1, :], lift2[last][:], ACT.Exp)
         for cases in halves:
             drop(last, cases)
 

@@ -87,9 +87,11 @@ def tile_picked_ycox_nll_p_kernel(
         nc.vector.tensor_copy(picked_scale[:], scale_table[:].indirect(offs_sb[:]))
         for j in range(PACK):
             rows = slice(QUADRANT + PACK * j, 3 * QUADRANT, PACK * PACK)
-            nc.sync.dma_start(out=x_scale[j:P:QUADRANT, :].bitcast(I32), in_=picked_scale[rows, :].bitcast(I32))
+            nc.scalar.dma_start(out=x_scale[j:P:QUADRANT, :].bitcast(I32), in_=picked_scale[rows, :].bitcast(I32))
         w_bf0 = keep.tile([P, P, PACK], BF16, name="w_bf0", align_bytes=64)
-        nc.vector.tensor_copy(*cast_views(w_bf0, first))
+        rounded, raw = cast_views(w_bf0, first)
+        nc.scalar.activation(rounded[:, :, : PACK // 2, :], raw[:, :, : PACK // 2, :], ACT.Copy)
+        nc.vector.tensor_copy(rounded[:, :, PACK // 2 :, :], raw[:, :, PACK // 2 :, :])
         w_bf1 = shared.tile([P, P, PACK], BF16, name="w_bf1", align_bytes=64, offset=SCALE_TABLE_AT)
         nc.vector.tensor_copy(*cast_views(w_bf1, last))
         quantise_w(w_bf0, first)

import math
from contextlib import ExitStack

import concourse.mybir as mybir

K, T, S, V, N, D = 512, 2048, 512, 256, 256, 2
P = 128
PACK = 4
QUADRANT = 32
LIST_ROWS = 16
QUARTER = S // 4
LINE_COLUMNS = 4
BANK_BYTES = 2048
CAP_BITS = 40
CAP = CAP_BITS * math.log(2.0)
FLOPS = 2 * K * N * S

F32 = mybir.dt.float32
BF16 = mybir.dt.bfloat16
I32 = mybir.dt.int32
U32 = mybir.dt.uint32
U16 = mybir.dt.uint16
U8 = mybir.dt.uint8
FP8X4 = mybir.dt.float8_e4m3fn_x4
ALU = mybir.AluOpType
ACT = mybir.ActivationFunctionType

SCALE_TABLE_AT = 0


def tile_picked_ycox_nll_p_kernel(
    tc, x_words, x_scales, w1, wgt, offs, case, pos1, pos2, out
):
    nc = tc.nc
    blocks = range(N // P)
    first, last = blocks[0], blocks[-1]
    with ExitStack() as ctx:
        keep = ctx.enter_context(tc.tile_pool(name="keep", bufs=1))
        psum = ctx.enter_context(tc.psum_pool(name="psum", bufs=1))
        shared = ctx.enter_context(tc.tile_pool(name="shared", bufs=1))

        scale_table = shared.tile([P, T], U8, name="scale_table", align_bytes=64, offset=SCALE_TABLE_AT)
        nc.vector.memset(scale_table[:].bitcast(I32), 0)
        x_scale = keep.tile([P, S], U8, name="x_scale", align_bytes=64)
        nc.vector.memset(x_scale[:].bitcast(I32), 0)
        w_raw = keep.tile([P, PACK, N], F32, name="w_raw")
        w_rows = w1.rearrange("(p t) m -> p t m", t=PACK)
        nc.sync.dma_start(out=w_raw[:, : PACK // 2, :], in_=w_rows[:, : PACK // 2, :])
        offs_sb = keep.tile([P, S // LIST_ROWS], U16, name="offs_sb")
        nc.sync.dma_start(offs_sb[:], offs)
        nc.sync.dma_start(
            out=scale_table[QUADRANT : 3 * QUADRANT : PACK, :].bitcast(I32), in_=x_scales[0].bitcast(I32)
        )
        nc.sync.dma_start(out=w_raw[:, PACK // 2 :, :], in_=w_rows[:, PACK // 2 :, :])
        word_table = keep.tile([P, T], U32, name="word_table", align_bytes=64)
        nc.sync.dma_start(
            out=word_table[:].bitcast(I32),
            in_=x_words[0].rearrange("p c t -> p (c t)").bitcast(I32),
        )
        pos2_sb = keep.tile([P, V // LIST_ROWS], U16, name="pos2_sb")
        nc.sync.dma_start(pos2_sb[:], pos2)
        case_sb = keep.tile([P, V // LIST_ROWS], U16, name="case_sb")
        nc.sync.dma_start(case_sb[:], case)
        pos1_sb = keep.tile([P, V // LIST_ROWS], U16, name="pos1_sb")
        nc.sync.dma_start(pos1_sb[:], pos1)

        w_code = [
            keep.tile([P, P], U32, name="w_code0", align_bytes=64),
            keep.tile([P, P], U32, name="w_code1", align_bytes=64),
        ]
        w_scale = [keep.tile([P, P], U8, name="w_scale%d" % b, align_bytes=64) for b in blocks]

        def cast_views(w_bf, b):
            return (
                w_bf[:].rearrange("p (c i) t -> p c t i", i=LINE_COLUMNS),
                w_raw[:, :, b * P : (b + 1) * P].rearrange("p t (c i) -> p c t i", i=LINE_COLUMNS),
            )

        def quantise_w(w_bf, b):
            nc.vector.quantize_mx(
                out=w_code[b][:].bitcast(FP8X4),
                scales=w_scale[b][:],
                in_=w_bf[:].rearrange("p m t -> p (m t)"),
            )

        picked_scale = keep.tile([P, S], U8, name="picked_scale", align_bytes=64, tag="weights")
        nc.vector.tensor_copy(picked_scale[:], scale_table[:].indirect(offs_sb[:]))
        for j in range(PACK):
            rows = slice(QUADRANT + PACK * j, 3 * QUADRANT, PACK * PACK)
            nc.scalar.dma_start(out=x_scale[j:P:QUADRANT, :].bitcast(I32), in_=picked_scale[rows, :].bitcast(I32))
        w_bf0 = keep.tile([P, P, PACK], BF16, name="w_bf0", align_bytes=64)
        rounded, raw = cast_views(w_bf0, first)
        nc.scalar.activation(rounded[:, :, : PACK // 2, :], raw[:, :, : PACK // 2, :], ACT.Copy)
        nc.vector.tensor_copy(rounded[:, :, PACK // 2 :, :], raw[:, :, PACK // 2 :, :])
        w_bf1 = shared.tile([P, P, PACK], BF16, name="w_bf1", align_bytes=64, offset=SCALE_TABLE_AT)
        nc.vector.tensor_copy(*cast_views(w_bf1, last))
        quantise_w(w_bf0, first)
        quantise_w(w_bf1, last)

        x_code = shared.tile([P, S], U32, name="x_code", align_bytes=64, offset=SCALE_TABLE_AT + T // 2)
        quarters = [slice(q * QUARTER, (q + 1) * QUARTER) for q in range(S // QUARTER)]
        for cols in quarters:
            entries = slice(cols.start // LIST_ROWS, cols.stop // LIST_ROWS)
            nc.vector.tensor_copy(x_code[:, cols], word_table[:].indirect(offs_sb[:, entries]))

        y = [keep.tile([P, S], F32, name="y%d" % b) for b in blocks]

        def product(bank, b, cols):
            acc = psum.tile([P, cols.stop - cols.start], F32, name="acc%d" % bank, offset=bank * BANK_BYTES)
            nc.tensor.matmul_mx(
                out=acc[:],
                lhsT=w_code[b][:].bitcast(FP8X4),
                lhsT_scale=w_scale[b][:],
                rhs=x_code[:, cols].bitcast(FP8X4),
                rhs_scale=x_scale[:, cols],
                start=True,
                stop=True,
            )
            return y[b][:, cols], acc[:]

        for q, cols in enumerate(quarters):
            for b in blocks:
                made = product(len(blocks) * q + b, b, cols)
                if b == last and cols == quarters[-2]:
                    nc.vector.tensor_copy(*made)
                else:
                    nc.scalar.activation(*made, ACT.Copy)
        weights = keep.tile([P, D, V], F32, name="weights", align_bytes=64)
        nc.sync.dma_start(out=weights[:], in_=wgt.rearrange("d p v -> p d v"))

        def case_tile(label):
            return keep.tile([P, V], F32, name=label)

        yc = [case_tile("yc%d" % b) for b in blocks]
        y2 = [case_tile("y2_%d" % b) for b in blocks]
        lift1 = [case_tile("lift1_%d" % b) for b in blocks]
        lift2 = [case_tile("lift2_%d" % b) for b in blocks]
        exps = [
            keep.tile([P, D, V], F32, name="exps%d" % b) for b in blocks
        ]
        halves = [slice(0, V // 2), slice(V // 2, V)]

        def drop(b, cases):
            nc.vector.scalar_tensor_tensor(
                exps[b][:, 0, cases], lift2[b][:, cases], CAP, lift1[b][:, cases], ALU.max, ALU.subtract
            )
            nc.scalar.activation(exps[b][:, 0, cases], exps[b][:, 0, cases], ACT.Exp, scale=-1.0)

        nc.vector.tensor_copy(y2[first][:], y[first][:].indirect(pos2_sb[:]))
        for cases in halves:
            entries = slice(cases.start // LIST_ROWS, cases.stop // LIST_ROWS)
            nc.scalar.activation(yc[first][:, cases], y[first][:].indirect(case_sb[:, entries]), ACT.Copy)
            nc.vector.tensor_tensor(
                lift1[first][:, cases], y[first][:].indirect(pos1_sb[:, entries]), yc[first][:, cases], ALU.subtract
            )
        nc.scalar.activation(yc[last][:], y[last][:].indirect(case_sb[:]), ACT.Copy)
        nc.vector.tensor_tensor(lift2[first][:], y2[first][:], yc[first][:], ALU.subtract)
        nc.scalar.activation(y2[last][:], y[last][:].indirect(pos2_sb[:]), ACT.Copy)
        early, late = halves
        y1_late = keep.tile([P, V // 2], F32, name="y1_late")
        nc.scalar.activation(y1_late[:], y[last][:].indirect(pos1_sb[:, late.start // LIST_ROWS :]), ACT.Copy)
        nc.vector.tensor_tensor(
            lift1[last][:, early],
            y[last][:].indirect(pos1_sb[:, : early.stop // LIST_ROWS]),
            yc[last][:, early],
            ALU.subtract,
        )
        nc.scalar.activation(exps[first][:, 1, :], lift2[first][:], ACT.Exp)
        drop(first, slice(0, V))
        nc.vector.tensor_tensor(lift2[last][:], y2[last][:], yc[last][:], ALU.subtract)
        nc.vector.tensor_tensor(lift1[last][:, late], y1_late[:], yc[last][:, late], ALU.subtract)
        nc.scalar.activation(exps[last][:, 1, :], lift2[last][:], ACT.Exp)
        for cases in halves:
            drop(last, cases)

        terms = [keep.tile([P, D, V], F32, name="terms%d" % b) for b in blocks]
        controls = [case_tile("controls%d" % b) for b in blocks]
        for b in blocks:
            nc.vector.scalar_tensor_tensor(terms[b][:], exps[b][:], 2.0**CAP_BITS, weights[:], ALU.min, ALU.mult)
        for b in blocks:
            nc.vector.scalar_tensor_tensor(
                controls[b][:], terms[b][:, 1, :], 2.0**-CAP_BITS, terms[b][:, 0, :], ALU.mult, ALU.add
            )
        top = [exps[b][:, 0, :] for b in blocks]
        for b in blocks:
            nc.vector.scalar_tensor_tensor(top[b], lift1[b][:], -CAP, lift2[b][:], ALU.add, ALU.max)
        for b in blocks:
            log_sum = case_tile("log_sum%d" % b)
            result = case_tile("result%d" % b)
            for cases in halves:
                nc.scalar.activation(log_sum[:, cases], controls[b][:, cases], ACT.Ln, bias=2.0**-CAP_BITS)
                nc.vector.scalar_tensor_tensor(
                    result[:, cases], top[b][:, cases], CAP, log_sum[:, cases], ALU.max, ALU.add
                )
            nc.sync.dma_start(out=out[b * P : (b + 1) * P, :], in_=result[:])
